import numpy as np, ml_dtypes
CORES = [3,11,19,27,35,43,51,59]
N = 8
import mx_ref
BF = ml_dtypes.bfloat16
def pick(q, e):
    c = np.concatenate([q[0].reshape(128, -1, 4), np.zeros((128, 1, 4), np.uint8)], axis=1); s = np.concatenate([q[1], np.ones((16, 1), np.uint8)], axis=1)
    return (np.ascontiguousarray(c[:, e].reshape(128, -1)), np.ascontiguousarray(s[:, e]))
def join(*qs):
    return (np.concatenate([q[0] for q in qs], axis=1), np.concatenate([q[1] for q in qs], axis=1))
def put(q, e, v):
    c, s = q[0].reshape(128, -1, 4).copy(), q[1].copy(); c[:, e] = v[0].reshape(128, -1, 4); s[:, e] = v[1]
    return (c.reshape(128, -1), s)
def pk(c, s):
    return (np.ascontiguousarray(c), mx_ref.live(s))
def emit(q):
    return q[0], q[1]
def decode(q):
    o = []
    for b in range(4):
        e = np.zeros((128, 128, 4), np.float32); e[np.arange(128), np.arange(128), b] = 1
        o.append(mx_ref.matmul(mx_ref.quantize(e.reshape(128, 512).astype(BF)), q))
    return np.stack(o, axis=2).reshape(128, -1)
def cut(t, i, w=512):
    return t[:, w * i:w * i + w]
def f(rng, *shape):
    return mx_ref.flush((rng.standard_normal(shape, dtype=np.float32) * np.exp2(rng.integers(-2, 3, shape[:-1] + (1,)))).astype(BF))
def wide(rng, *shape, cols=0):
    v = rng.standard_normal(shape, dtype=np.float32) * np.exp2(rng.integers(-12, 13, shape)).astype(np.float32)
    if cols: v *= np.repeat(np.exp2(rng.integers(-cols, cols + 1, shape[:-2] + (1, shape[-1] // 4))) * (rng.random(shape[:-2] + (1, shape[-1] // 4)) > 0.0625), 4, axis=-1).astype(np.float32)
    return mx_ref.flush(v.astype(BF))
C, T, M, R, G, O = 32, 256, 16, 3, 4, 2
def big(v):
    v = v.astype(np.float32)
    return np.where(np.abs(v) < np.float32(2.0 ** -16), np.float32(0), v).astype(BF)
def signed(rng, *shape):
    return (1 + rng.random(shape)) * rng.choice([-1.0, 1.0], shape)
def tiles(v):
    return np.ascontiguousarray(v.reshape(N, 128, -1).astype(np.float32).astype(BF))
def setup_inputs(rng):
    return {"c": big(f(rng, N, 128, 4 * C)), "x": big(f(rng, N, 128, 4 * T)), "u": f(rng, N, 128, 16), "w": f(rng, N, 128, 512 * O)}
def setup_inputs_dark(rng):
    d = setup_inputs(rng)
    top = np.arange(128) < 64
    kind = np.stack([rng.permutation(T) for r in range(N)]) < 2 * T // 3
    on = kind[:, None, :] == top[None, :, None]
    d["x"] = tiles((1.75 + 0.25 * rng.random((N, 128, T, 4))) * on[:, :, :, None] * 2.0 ** 29)
    d["u"] = tiles((2 + 0.2 * rng.random((N, 128, 4, 4))) * 2.0 ** 28)
    c = 0.5 * signed(rng, N * C, 128, 4)
    b = M + rng.permutation(N * C - M)[:2 * M]
    for half, e in ((top, b[:M + M // 2]), (~top, b[M + M // 2:])):
        c[np.ix_(e, np.flatnonzero(half))] = 2.5 + 0.5 * rng.random((len(e), 64, 4))
    d["c"] = tiles(c.reshape(N, C, 128, 4).transpose(0, 2, 1, 3) * 2.0 ** 28)
    return d
def setup_inputs_low(rng):
    d = setup_inputs(rng)
    s = np.where(np.stack([rng.permutation(T) for r in range(N)]) < 3 * T // 4, 1.0, -1.0)
    d["x"] = tiles(np.exp2(2 * rng.random((N, 128, T, 4))) * s[:, None, :, None] * 2.0 ** 28)
    d["u"] = tiles((1.85 + 2 * rng.random((N, 128, 4, 4))) * 2.0 ** 28)
    d["c"] = tiles((1.9 + 2 * rng.random((N, 128, C, 4)) + 0.1 * rng.random((N, 1, C, 1))) * 2.0 ** 28)
    return d
def setup_inputs_near(rng):
    d = setup_inputs(rng)
    c, x, u = np.zeros((N, 128, C, 4)), np.zeros((N, 128, T, 4)), np.zeros((N, 128, 4, 4))
    same = signed(rng, 64, 4)
    c[:, :64] = signed(rng, N, 64, C, 4)
    c[:, 80:88] = signed(rng, N, 8, C, 4) * 2.0 ** -3
    c[:, 112, :, 0] = 40
    c[:, 120, :, 0] = 0.25
    a, e = int(rng.integers(0, N)), rng.permutation(C)[:M]
    c[a][:64, e] = same[:, None, :]
    u[:, :64, 0] = same
    u[:, 112, 0, 0] = 40
    for r in range(N):
        h = rng.permutation(T) // 4
        i = np.zeros(T)
        i[np.argsort(h, kind="stable")] = np.arange(T) % 4 == 3
        x[r, :64] = signed(rng, 64, T // 4, 4)[:, h]
        x[r, 64:72] = signed(rng, 8, T, 4) * 2.0 ** -11
        x[r, 112, :, 0] = 40
        x[r, 120, :, 0] = (1 + i) * 2.0 ** -11
    d["c"], d["x"], d["u"] = tiles(c * 2.0 ** -4), tiles(x * 2.0 ** -4), tiles(u * 2.0 ** -4)
    return d
def setup_inputs_ties(rng):
    d = setup_inputs(rng)
    c, x, u = np.zeros((N, 128, C, 4)), np.zeros((N, 128, T, 4)), np.zeros((N, 128, 4, 4))
    h = rng.permutation(N * C) // (M // 2 + 3)
    p = signed(rng, 64, int(h.max()) + 1, 4)
    u[:, :64, 0] = p[:, 0]
    for r in range(N):
        c[r, :64] = p[:, h[C * r:C * r + C]]
        g = rng.permutation(T) // 4
        x[r, :64] = signed(rng, 64, T // 4, 4)[:, g]
        x[r, 64:] = signed(rng, 64, T, 4)
    d["c"], d["x"], d["u"] = tiles(c), tiles(x), tiles(u)
    return d
def setup_inputs_spread(rng):
    return {"c": big(wide(rng, N, 128, 4 * C, cols=6)), "x": big(wide(rng, N, 128, 4 * T, cols=6)), "u": wide(rng, N, 128, 16), "w": wide(rng, N, 128, 512 * O)}
def check_inputs(d):
    b = []
    for k, low in (("c", -16), ("x", -16), ("u", -30), ("w", -30)):
        v = np.abs(d[k].astype(np.float32))
        if not (np.isfinite(v).all() and ((v == 0) | (v >= 2.0 ** low) & (v <= 2.0 ** 30)).all()): b.append("a value of " + k)
    return b
def reference(c, x, u, w):
    every = join(*[mx_ref.quantize(np.ascontiguousarray(c[q])) for q in range(N)])
    tok = [mx_ref.quantize(np.ascontiguousarray(x[r])) for r in range(N)]
    s, mark = [], []
    for r in range(N):
        s.append(np.concatenate([mx_ref.matmul(pick(every, np.arange(i, i + 128)), tok[r]) for i in range(0, N * C, 128)]) + np.float32(0))
        a = np.concatenate([u[r], np.zeros((128, 496), BF)], axis=1)
        mark.append(mx_ref.matmul(mx_ref.quantize(a), tok[r])[0] + np.float32(0))
    free, won, made = np.ones(N * C, bool), [], []
    for t in range(R):
        gain = np.zeros(N * C, int)
        for r in range(N): gain = gain + np.sum(s[r] > mark[r], axis=1)
        win = np.argsort(np.where(free, -gain, 1), kind="stable")[:M]
        free[win] = False
        named = [np.argmax(s[r][win] - mark[r], axis=1) for r in range(N)]
        v = decode(pick(every, win))
        for i in range(G):
            v = (v + decode(join(*[pick(tok[(k + i) % N], named[(k + i) % N][k:k + 1]) for k in range(M)]))) * np.float32(0.5)
        q = mx_ref.quantize(np.ascontiguousarray(v.astype(BF)))
        full = pick(q, np.concatenate([np.arange(M), np.full(128 - M, -1)]))
        for r in range(N):
            z = mx_ref.matmul(full, tok[r])[:M] + np.float32(0)
            mark[r] = np.maximum(mark[r], np.max(z, axis=0))
        won.append(win)
        made.append(q)
    q = join(*made)
    n = R * M
    y, oc, osc = np.zeros((N, 128, O * n), np.float32), np.zeros((N, 128, 4 * n), np.uint8), np.zeros((N, 16, n), np.uint8)
    sel, mk = np.zeros((N, 1, n), np.float32), np.zeros((N, 1, T), np.float32)
    for r in range(N):
        for o in range(O): y[r, :, o * n:o * n + n] = mx_ref.matmul(mx_ref.quantize(np.ascontiguousarray(cut(w[r], o))), q)
        oc[r], osc[r] = emit(q)
        sel[r, 0] = np.concatenate(won)
        mk[r, 0] = mark[r]
    return {"y": y, "oc": oc, "osc": osc, "sel": sel, "mk": mk}

@@ -1,0 +1,501 @@
+from concourse.bass import DstId, RemoteDMATransfer
+from concourse.mybir import dt, AluOpType as ALU, AxisListType, ActivationFunctionType as AF
+
+M, R, O = 16, 3, 2
+BFT, F32, I32, U16, COD, PLN = "bfloat16", "float32", "int32", "uint16", "float8_e4m3fn_x4", "uint8"
+SCRATCH = {}
+
+
+def _sb(name, n, d):
+    SCRATCH[name] = ("sbuf", [128, n], d)
+
+
+def _codes(name, n):
+    _sb(name + "q", n, COD)
+    _sb(name + "s", n, PLN)
+
+
+for _n, _w in (("ctile", 512), ("zt", 512), ("xt", 1024), ("xu", 1024), ("wt", 1024), ("h", 512), ("ind", 512), ("tab", 2048),
+               ("kt", 1024), ("oh", 512), ("ohn", 512), ("nm", 520), ("eb", 2048), ("wgt", 512), ("gmask", 8),
+               ("ones", 128), ("ident", 128), ("place", 128), ("placen", 16), ("sg", 128), ("junk0", 256), ("junk1", 256)):
+    _sb(_n, _w, BFT)
+for _n, _w in (("mrow", 256), ("d0", 256), ("d1", 256), ("run0", 256), ("run1", 256), ("kcol", 2), ("cap", 2), ("o16", 2),
+               ("tot", 2), ("md", 3), ("step", 7), ("fac", 80), ("low", 16), ("sq", 128),
+               ("vrow", 80), ("vblk", 160), ("vtr", 160), ("yt", 96), ("selrow", 48), ("name", 2), ("won", 2)):
+    _sb(_n, _w, F32)
+for _t in range(R):
+    _sb("rk%d" % _t, 2, F32)
+for _t in range(2):
+    _sb("mk%d" % _t, 96, F32)
+    _sb("mt%d" % _t, 64, F32)
+for _n, _w in (("pn", 2), ("pl", 2), ("ph", 2), ("vi", 80), ("vi2", 80), ("v16", 16)):
+    _sb(_n, _w, I32)
+_sb("offv", 6, U16)
+_sb("offk", 16, U16)
+_sb("offo", 2, U16)
+for _t in range(R):
+    _sb("off%d" % _t, 4, U16)
+    _sb("cnt%d" % _t, 2, BFT)
+    _sb("land%d" % _t, 14, BFT)
+    _codes("win%d" % _t, 144)
+    _codes("v%d" % _t, 128)
+for _n, _w in (("c", 128), ("call", 256), ("x", 256), ("xu", 256), ("w", 256), ("vu", 128), ("vo", 48), ("ind", 128), ("kt", 256),
+               ("oh", 128), ("ohn", 128), ("nm", 130), ("eb", 512), ("wgt", 128), ("vin", 128)):
+    _codes(_n, _w)
+for _b in range(8):
+    SCRATCH["ps%d" % _b] = ("psum", [128, 512], F32)
+SEMAPHORES = ["rc"] + ["rn%d" % t for t in range(R)] + ["rt%d" % t for t in range(R)] + ["ls"] + ["e%d" % i for i in range(140)]
+
+
+def _add(P, q, name, fn, r=(), w=(), inc=1, ext=None):
+    ops, tags = P["ops"], P["tags"]
+    i = len(ops)
+    deps = set()
+    if q == "G" and name[:3] != "snd":
+        w = list(w) + ["pool"]
+    for t in r:
+        s = tags.setdefault(t, {"w": None, "r": []})
+        if s["w"] is not None:
+            deps.add(s["w"])
+        if t[0] == "B":
+            deps.update(j for j in s["r"] if ops[j]["q"] != q)
+    for t in w:
+        s = tags.setdefault(t, {"w": None, "r": []})
+        if s["w"] is not None:
+            deps.add(s["w"])
+        deps.update(s["r"])
+    for t in r:
+        tags[t]["r"].append(i)
+    for t in w:
+        tags[t]["w"] = i
+        tags[t]["r"] = []
+    deps.discard(i)
+    ops.append({"q": q, "name": name, "fn": fn, "deps": deps, "inc": inc, "ext": ext})
+
+
+def _emit(P, g, T):
+    queues = {"G": g, "V": g.vector, "A": g.scalar, "P": g.tensor, "S": g.sync}
+    ops = P["ops"]
+    known = {q: 0 for q in queues}
+    done, waits, used = [], [], set()
+    for i, o in enumerate(ops):
+        if o["ext"] is not None:
+            done.append(1 << i)
+            waits.append([])
+            continue
+        need = []
+        for j in sorted(o["deps"], reverse=True):
+            if not known[o["q"]] >> j & 1:
+                need.append(j)
+                known[o["q"]] |= done[j]
+        keep = [j for j in need if not any(done[m] >> j & 1 for m in need if m != j)]
+        waits.append(sorted(keep))
+        used.update(keep)
+        done.append(known[o["q"]] | 1 << i)
+    pool, val = [], {}
+    for i, o in enumerate(ops):
+        if o["ext"] is not None:
+            val[i] = o["ext"]
+            continue
+        q = queues[o["q"]]
+        for j in waits[i]:
+            q.wait_ge(*val[j])
+        if o["fn"] is None:
+            continue
+        ins = o["fn"](q)
+        if i in used:
+            dma = o["inc"] > 1
+            free = [s for s in pool if not dma and not s["dma"] and done[i] >> s["last"] & 1]
+            free.sort(key=lambda s: -s["last"])
+            if free:
+                s = free[0]
+            else:
+                s = {"sem": T.sem["e%d" % len(pool)], "n": 0, "dma": dma}
+                pool.append(s)
+            s["last"] = i
+            s["n"] += o["inc"]
+            ins.then_inc(s["sem"], o["inc"])
+            val[i] = (s["sem"], s["n"])
+
+
+def rank_program(g, core, T, topo):
+    r = T.rank_of(core)
+    if r is None:
+        return
+    cores = list(T.cores)
+    N = len(cores)
+    P = {"ops": [], "tags": {}}
+    chip = [topo.chip(q) for q in cores]
+    ways = {"far": [], "plane": [], "mate": []}
+    for d in range(1, N):
+        q = r ^ d
+        way = "mate" if topo.mates(chip[r], chip[q]) else "plane" if topo.same_plane(chip[r], chip[q]) else "far"
+        ways[way].append(q)
+    others = []
+    while ways["far"] or ways["plane"]:
+        for way in ("far", "plane"):
+            others += ways[way][:1]
+            del ways[way][:1]
+    others += ways["mate"]
+    mask = 0xFFFF
+    for q in others:
+        mask &= topo.mask(core, cores[q])
+    lanes = len([e for e in topo.engines(core, cores[others[0]]) if mask >> e & 1])
+    sent = [0]
+
+    def op(*a, **k):
+        _add(P, *a, **k)
+
+    def u8(ap):
+        return ap.bitcast(dt.uint8)
+
+    def w32(ap):
+        return ap.bitcast(dt.uint32)
+
+    def slot(src, dst):
+        return (src - dst) % N
+
+    def send(name, reads, src, dst, sem):
+        ids = []
+        for q in others:
+            rid, pid, _ = topo.addr(cores[q])
+            ids.append(DstId(rid=rid, pnc=pid))
+        dsts = [dst(q) for q in others]
+        sent[0] += lanes
+        op("G", name, lambda e: e.remote_dma_fused([RemoteDMATransfer(dst_ids=ids, dma_engine_mask=mask, remote_sem=T.sem[sem],
+                                                                      srcs=[src], dsts=dsts)], local_sem=T.sem.ls), r=reads)
+
+    def memset(name, ap, v, w):
+        op("V", name, lambda e: e.memset(ap, v), w=w)
+
+    def quant(name, out, c0, tile, a, n, r, w):
+        op("V", name, lambda e: e.quantize_mx(T[out + "q"][:, c0:c0 + n], T[out + "s"][:, c0:c0 + n], T[tile][:, a:a + 4 * n]), r=r, w=w)
+
+    def mm(name, bank, st, a, mv, b, n, r, start=True, stop=True):
+        op("P", name, lambda e: e.matmul_mx(T["ps%d" % bank][:, 0:n], T[st + "q"][:, a:a + 128], T[st + "s"][:, a:a + 128],
+                                            T[mv + "q"][:, b:b + n], T[mv + "s"][:, b:b + n], start, stop), r=r, w=["B%d" % bank])
+
+    def ps(bank, a, b):
+        return T["ps%d" % bank][:, a:b]
+
+    def ts(name, out, in0, s1, s2, o0, o1, r, w):
+        if o1 is None:
+            op("V", name, lambda e: e.tensor_scalar(out, in0, s1, None, o0), r=r, w=w)
+        else:
+            op("V", name, lambda e: e.tensor_scalar(out, in0, s1, s2, o0, o1), r=r, w=w)
+
+    def tt(name, out, in0, in1, o, r, w):
+        op("V", name, lambda e: e.tensor_tensor(out, in0, in1, o), r=r, w=w)
+
+    def vcopy(name, out, in_, r, w):
+        op("V", name, lambda e: e.tensor_copy(out, in_), r=r, w=w)
+
+    def acopy(name, out, in_, r, w, **k):
+        op("A", name, lambda e: e.activation(out, in_, AF.Copy, **k), r=r, w=w)
+
+    def load(q, name, out, in_, r=(), w=()):
+        op(q, name, lambda e: e.dma_start(out, in_), r=r, w=w, inc=16)
+
+    order = [None] * M
+    for k in range(M):
+        i, h = (r - k) % N, k // N
+        order[(i % 4) + 4 * h + 8 * (i // 4)] = k
+    place_of = {k: j for j, k in enumerate(order)}
+    HT = ["h0", "h1", "h2", "h3"]
+    EB = ["eb0", "eb1", "eb2", "eb3"]
+    PL = ["place%d" % j for j in range(M)]
+    RND = 1.5 * 2.0 ** 27
+    CV = 96
+    NV = 5 * M
+
+    load("S", "ldc", T.ctile[:, 0:128], T.c[:, :], w=["ctile"])
+    load("A", "ldx", T.xt[:, :], T.x[:, :], w=["xt"])
+    memset("ms_c", T.ctile[:, 128:512], 0.0, ["ctile0"])
+    memset("ms_ones", T.ones[:], 1.0, ["ones"])
+    memset("ms_h", T.h[:], 0.0, HT + ["hu", "hc0", "hc1"])
+    memset("ms_h1", T.h[:, 4 * CV:4 * CV + 2], 1.0, ["hc0"])
+    memset("ms_h2", T.h[:, 4 * CV + 6:4 * CV + 8], 1.0, ["hc1"])
+    load("S", "ldu", T.h[:, 4 * NV:4 * NV + 4], T.u[:, 0:4], w=["hu"])
+    memset("ms_zt", T.zt[:], 0.0, ["zt"])
+    op("G", "pn", lambda e: e.iota(T.pn[:], [[128, 2]], 0, 1), w=["pn"])
+    op("G", "vi", lambda e: e.iota(T.vi[:], [[4, 2], [16, 8], [17, 5]], 256 - 17 - 16 * r, 0), w=["vi"])
+    op("G", "v16", lambda e: e.iota(T.v16[:], [[1, 16]], 0, 0), w=["v16"])
+    op("G", "ident", lambda e: e.affine_select(T.ident[:], T.ones[:], [[-1, 128]], ALU.is_equal, 0.0, 0, 1), r=["ones"], w=["ident"])
+
+    quant("qc", "c", 0, "ctile", 0, 128, ["ctile", "ctile0"], ["c"])
+    send("snd_cq", ["c"], u8(T.cq[:, 0:32]), lambda q: u8(T.callq[:, 32 * r:32 * r + 32]), "rc")
+    send("snd_cs", ["c"], T.cs[:, 0:32], lambda q: T.calls[:, 32 * r:32 * r + 32], "rc")
+    load("S", "ownq", u8(T.callq[:, 32 * r:32 * r + 32]), u8(T.cq[:, 0:32]), r=["c"], w=["own.q"])
+    load("S", "owns", T.calls[:, 32 * r:32 * r + 32], T.cs[:, 0:32], r=["c"], w=["own.s"])
+    op("X", "arr_c", None, w=["call"], ext=(T.sem.rc, 2 * lanes * (N - 1)))
+    CALL = ["call", "own.q", "own.s"]
+
+    for j in range(M):
+        acopy("place", T.place[:, j:128:16], T.ones[:, 0:8], ["ones"], [PL[j]], scale=255.0 - 2.0 * order[j])
+    memset("ms_kt", T.kt[:], 0.0, ["kta", "ktb", "kto0", "kto1", "ktr0", "ktr1", "ktc", "ktd"])
+    for t in range(2):
+        memset("ms_mk%d" % t, T["mk%d" % t][:, 32:96], 0.0, ["mk%d.0" % t, "mk%d.1" % t])
+    for a in range(4):
+        for b in range(2):
+            (vcopy if b else acopy)("xu", T.xu[:, 512 * b + 128 * a:512 * b + 128 * a + 128], T.xt[:, 256 * a + 128 * b:256 * a + 128 * b + 128],
+                                    ["xt"], ["xu%d%d" % (a, b)])
+    quant("qv", "vu", 0, "h", 0, 128, HT + ["hu", "hc0", "hc1"], ["vu"])
+    quant("qxu", "xu", 0, "xu", 0, 256, ["xu%d%d" % (a, b) for a in range(4) for b in range(2)], ["xuq"])
+    acopy("z_nm", T.nm[:, 0:512], T.zt[:], ["zt"], ["nm", "nmlo", "nmhi"])
+    acopy("z_oh", T.oh[:], T.zt[:], ["zt"], ["oh0", "oh1"])
+    ts("pl", T.pl[:], T.pn[:], 15, None, ALU.bitwise_and, None, ["pn"], ["pl"])
+    ts("vi2", T.vi2[:], T.vi[:], 127, None, ALU.bitwise_and, None, ["vi"], ["vi2"])
+    for d in range(3):
+        ts("md", T.md[:, d:d + 1], T.pl[:, 0:1], 3.0 + d, None, ALU.is_equal, None, ["pl"], ["md%d" % d])
+    vcopy("vrow", T.vrow[:], T.vi2[:], ["vi2"], ["vrow"])
+    for k in range(7):
+        acopy("step", T.step[:, k:k + 1], T.md[:, 1 + k // 4:2 + k // 4], ["md%d" % (1 + k // 4)], ["step%d" % k], scale=16.0 * 2 ** k)
+    quant("qx", "x", 0, "xt", 0, 256, ["xt"], ["x"])
+    memset("ms_wgt", T.wgt[:], 256.0, ["wgt"])
+    memset("ms_wgt", T.wgt[:, 2:512:4], 1.0, ["wgt"])
+    op("G", "ktc", lambda e: e.iota(T.kt[32:33, 2:1024:4], [[0, 16], [-1, 16]], 15, 0, allow_small_or_imprecise_dtypes=True), w=["ktc", "ktc2"])
+    op("G", "ktd", lambda e: e.iota(T.kt[64:65, 2:1024:4], [[-16, 16], [0, 16]], 240, 0, allow_small_or_imprecise_dtypes=True),
+       w=["ktd", "ktd2", "ktd3"])
+    op("G", "gmask0", lambda e: e.affine_select(T.gmask[:], T.ones[:, 0:8], [[-16, 8]], ALU.is_ge, 0.0, 0, 1), r=["ones"], w=["gmask"])
+    op("G", "gmask1", lambda e: e.affine_select(T.gmask[:], T.gmask[:], [[16, 8]], ALU.is_ge, 0.0, 15, -1), r=["gmask"], w=["gmask"])
+
+    def zmul(v):
+        for b in range(2):
+            mm("z%d" % b, 4 + b, "xu", 128 * b, v, 0, 128, ["xuq", v])
+
+    def mk(t, b):
+        return T["mk%d" % (t % 2)][:, 32 * b + 32:32 * b + 33]
+
+    def marks(t, b):
+        q = "mk%d.%d" % (t % 2, b)
+        if t == 0:
+            vcopy("mark%d" % b, mk(0, b), ps(4 + b, NV, NV + 1), ["B%d" % (4 + b)], [q])
+        else:
+            op("V", "mark%d" % b, lambda e: e.tensor_tensor_scan(T["mk%d" % (t % 2)][:, 32 * b + 33 - M:32 * b + 33], T["ps%d" % (4 + b)][:, 4:NV:5],
+                                                                 T.low[:], mk(t - 1, b), ALU.max, ALU.max),
+               r=["B%d" % (4 + b), "low", "mk%d.%d" % ((t - 1) % 2, b)], w=[q])
+
+    def turn(t):
+        op("V", "turn", lambda e: e.transpose(T["mt%d" % (t % 2)][:], T["mk%d" % (t % 2)][:, 32:96]),
+           r=["mk%d.0" % (t % 2), "mk%d.1" % (t % 2)], w=["mt%d" % (t % 2)])
+
+    def spread(t, aa):
+        for a in aa:
+            op("G", "spread%d" % a, lambda e, a=a: e.partition_broadcast(T.mrow[:, 64 * a:64 * a + 64], T["mt%d" % (t % 2)][32 * a:32 * a + 1, :], 128),
+               r=["mt%d" % (t % 2)], w=["mrow%d" % a])
+
+    zmul("vu")
+    marks(0, 0)
+    marks(0, 1)
+    quant("qwgt", "wgt", 0, "wgt", 0, 128, ["wgt"], ["wgtq"])
+    turn(0)
+    spread(0, (0, 1, 2, 3))
+    ts("tab", T.tab[:, 0:16], T.v16[:], T.md[:, 0:1], None, ALU.mult, None, ["v16", "md0"], ["tab0"])
+    memset("ms_cap", T.cap[:], 256.0, ["cap"])
+    for k in range(5):
+        m = 16 << k
+        ts("tab", T.tab[:, m:2 * m], T.tab[:, 0:m], T.step[:, k:k + 1], None, ALU.add, None, ["tab%d" % j for j in range(k + 1)] + ["step%d" % k], ["tab%d" % (k + 1)])
+    TOP = 256 * (N - 1) + 16
+    TAB = ["tab%d" % j for j in range(8)]
+    memset("kt32", T.kt[32:33, 130:1024:512], 0.0, ["ktc"])
+    memset("kt96", T.kt[96:97, 130:1024:512], 15.0, ["ktc2"])
+    memset("kt64", T.kt[64:65, 258:1024:512], 0.0, ["ktd"])
+    memset("kt96", T.kt[96:97, 258:259], 176.0, ["ktd2"])
+    memset("kt96", T.kt[96:97, 770:771], 48.0, ["ktd3"])
+    for k in range(M):
+        acopy("vrowk", T.vrow[:, 5 * k:5 * k + 1], T.ones[:, 0:1], ["vrow", "ones"], ["vrow.%d" % k], scale=float(128 + place_of[k]))
+    for k in (5, 6):
+        op("A", "tab", lambda e, m=16 << k, k=k: e.activation(T.tab[:, m:min(2 * m, TOP)], T.tab[:, 0:min(m, TOP - m)], AF.Identity, bias=T.step[:, k:k + 1]),
+           r=["tab%d" % j for j in range(k + 1)] + ["step%d" % k], w=["tab%d" % (k + 1)])
+
+    def above(t, b, k):
+        ts("above", T.ind[:, 2 * k + b:512:4], ps(b, 128 * k, 128 * k + 128), mk(t, b), None, ALU.is_gt, None,
+           ["B%d" % b, "mk%d.%d" % (t % 2, b)], ["ind%d%d" % (b, k)])
+
+    def above_a(t):
+        op("A", "sgn", lambda e: e.activation(T.sg[:], T.sq[:], AF.Sign, bias=mk(t, 0), scale=-1.0), r=["sq", "mk%d.0" % (t % 2)], w=["sg"])
+        op("A", "neg", lambda e: e.activation(T.ind[:, 2:512:4], T.sg[:], AF.Relu, scale=-1.0), r=["sg"], w=["ind01"])
+
+    def pieces(what, b, lo, hi):
+        return ["%s%d.%d" % (what, b, h) for h in range(lo // 64, hi // 64)]
+
+    def name_diff(b, lo, hi):
+        tt("diff%d" % b, T["d%d" % b][:, lo:hi], ps(2 + b, lo, hi), T.mrow[:, lo:hi], ALU.subtract,
+           ["B%d" % (2 + b)] + ["mrow%d" % a for a in range(lo // 64, hi // 64)], pieces("d", b, lo, hi))
+
+    def name_run(b, lo, hi):
+        first = T["run%d" % b][:, lo - 1:lo] if lo else -1e29
+        op("V", "run%d" % b, lambda e: e.tensor_tensor_scan(T["run%d" % b][:, lo:hi], T["d%d" % b][:, lo:hi], T["d%d" % b][:, lo:hi], first, ALU.max, ALU.max),
+           r=pieces("d", b, lo, hi) + (pieces("run", b, 0, lo) if lo else []), w=pieces("run", b, lo, hi))
+
+    def name_at(b):
+        op("A", "name%d" % b, lambda e: e.activation(T["junk%d" % b][:], T["run%d" % b][:], AF.Sign, bias=T["run%d" % b][:, 255:256], scale=-1.0,
+                                                     accum_out=T.name[:, b:b + 1]), r=pieces("run", b, 0, 256), w=["junk%d" % b, "name%d" % b])
+
+    def pick_out(t):
+        v = "v%d" % t
+        op("V", "outq", lambda e: e.tensor_copy(w32(T.voq[:, M * t:M * t + M]), w32(T[v + "q"][:, 0:128]).indirect(T.offo[:, 0:1])), r=[v, "offo"], w=["vo.q%d" % t])
+        op("A", "outs", lambda e: e.activation(T.vos[:, M * t:M * t + M], T[v + "s"][:, 0:128].indirect(T.offo[:, 0:1]), AF.Copy), r=[v, "offo"], w=["vo.s%d" % t])
+
+    def products(t):
+        v = "v%d" % t
+        for o in range(O):
+            mm("y%d" % o, 6 + o, "w", 128 * o, v, 0, 128, ["w", v])
+        for o in range(O):
+            (vcopy if o else acopy)("yc%d" % o, T.yt[:, R * M * o + M * t:R * M * o + M * t + M], T["ps%d" % (6 + o)][:, 4:NV:5],
+                                    ["B%d" % (6 + o)], ["yt%d%d" % (t, o)])
+
+    def one_round(t):
+        win, off, rk, cnt, land = "win%d" % t, "off%d" % t, "rk%d" % t, "cnt%d" % t, "land%d" % t
+        if t == 0:
+            for b in range(2):
+                mm("sb%d" % b, b, "xu", 128 * b, "call", 0, 256, ["xuq"] + CALL)
+            for b in range(2):
+                for k in range(2):
+                    above(t, b, k)
+        else:
+            marks(t, 0)
+            above_a(t)
+            above(t, 0, 0)
+            marks(t, 1)
+            turn(t)
+            above(t, 1, 0)
+            above(t, 1, 1)
+        quant("qind", "ind", 0, "ind", 0, 128, ["ind00", "ind01", "ind10", "ind11"], ["indq"])
+        if t:
+            spread(t, (0, 1))
+        mm("cnt", 6, "ind", 0, "vu", 0, 128, ["indq", "vu"])
+        vcopy("cnt", T[cnt][:], ps(6, CV, CV + 2), ["B6"], [cnt])
+        send("snd_n", [cnt], T[cnt][:], lambda q: T[land][:, 2 * slot(r, q) - 2:2 * slot(r, q)], "rn%d" % t)
+        op("X", "arr_n", None, w=[land], ext=(T.sem["rn%d" % t], lanes * (N - 1)))
+        ts("c16", T.o16[:], ps(6, CV, CV + 2), RND, RND, ALU.add, ALU.subtract, ["B6"], ["o16"])
+        tt("crest", T.won[:], ps(6, CV, CV + 2), T.o16[:], ALU.subtract, ["B6", "o16"], ["won"])
+        tt("ccap", T.o16[:], T.o16[:], T.cap[:], ALU.min, ["cap", "o16"], ["o16"])
+        for b in range(2):
+            acopy("own", T.kt[:, 512 * b + 3:512 * b + 512:4], T.ident[:], ["ident", "won"], ["ktr%d" % b], scale=T.won[:, b:b + 1])
+            acopy("own", T.kt[:, 512 * b + 1:512 * b + 512:4], T.ident[:], ["ident", "o16"], ["kto%d" % b], scale=T.o16[:, b:b + 1])
+        if t:
+            spread(t, (2, 3))
+        else:
+            op("G", "placen", lambda e: e.iota(T.placen[:], [[-2, 16]], 255, 0, allow_small_or_imprecise_dtypes=True), w=["placen"])
+            for b in range(2):
+                mm("sa%d" % b, 2 + b, "call", 128 * b, "x", 0, 256, ["x"] + CALL)
+        for lo, hi in (((0, 128), (128, 192), (192, 256)) if t else ((0, 256),)):
+            for b in range(2):
+                name_diff(b, lo, hi)
+            for b in range(2):
+                name_run(b, lo, hi)
+        name_at(0)
+        if t == 0:
+            for b in range(4):
+                load("S", "z_eb", T.eb[:, 512 * b:512 * b + 512], T.zt[:], r=["zt", land], w=[EB[b]])
+        if t == 1:
+            load("S", "ldw", T.wt[:, :], T.w[:, :], r=[land], w=["wt"])
+            load("S", "z_ohn", T.ohn[:], T.zt[:], r=["zt", land], w=["ohn"])
+        for b in range(2):
+            op("V", "tot", lambda e, b=b: e.tensor_reduce(T.tot[:, b:b + 1], T[land][:, b:14:2], AxisListType.X, ALU.add), r=[land], w=["tot%d" % b])
+        for b in range(2):
+            ts("offk", T.offk[:, 8 * b:8 * b + 8], T.gmask[:], T.tot[:, b:b + 1], None, ALU.mult, None, ["gmask", "tot%d" % b], ["offk%d" % b])
+        op("A", "gain1", lambda e: e.activation(T.kt[:, 512:1024:4], T.tab[:, 0:TOP].indirect(T.offk[:, 8:16]), AF.Copy), r=TAB + ["offk1"], w=["ktb"])
+        op("V", "gain0", lambda e: e.tensor_copy(T.kt[:, 0:512:4], T.tab[:, 0:TOP].indirect(T.offk[:, 0:8])), r=TAB + ["offk0"], w=["kta"])
+        name_at(1)
+        KC = ["ktc", "ktd", "ktc2", "ktd2", "ktd3"]
+        quant("qkta", "kt", 0, "kt", 0, 128, ["kta", "kto0", "ktr0"] + KC, ["ktqa"])
+        quant("qktb", "kt", 128, "kt", 512, 128, ["ktb", "kto1", "ktr1"] + KC, ["ktqb"])
+        mm("kcol0", 6, "kt", 0, "wgt", 0, 128, ["ktqa", "wgtq"])
+        mm("krow", 7, "wgt", 0, "kt", 0, 256, ["ktqa", "ktqb", "wgtq"])
+        mm("kcol1", 4, "kt", 128, "wgt", 0, 128, ["ktqb", "wgtq"])
+        if t == 0:
+            ts("ph", T.ph[:], T.pn[:], 240, None, ALU.bitwise_and, None, ["pn"], ["ph"])
+            vcopy("nm_l", T.nm[:, 0:2], T.pl[:], ["pl", "nm"], ["nm_l"])
+        vcopy("kcc0", T.kcol[:, 0:1], ps(6, 0, 1), ["B6"], ["kcol0"])
+        if t == 0:
+            vcopy("nm_h", T.nm[:, 8:10], T.ph[:], ["ph", "nm"], ["nm_h"])
+            memset("z_nm2", T.nm[:, 512:520], 0.0, ["nm2"])
+        ts("n16", T.nm[:, 24:26], T.name[:], RND, RND, ALU.add, ALU.subtract, ["name0", "name1", "nm"], ["nmhi"])
+        vcopy("kcc1", T.kcol[:, 1:2], ps(4, 0, 1), ["B4"], ["kcol1"])
+        tt("nrest", T.nm[:, 16:18], T.name[:], T.nm[:, 24:26], ALU.subtract, ["name0", "name1", "nmhi", "nm"], ["nmlo"])
+        quant("qnm", "nm", 0, "nm", 0, 130, ["nm", "nm2", "nm_l", "nm_h", "nmlo", "nmhi"], ["nmq"])
+        for b in range(2):
+            op("A", "rank%d" % b, lambda e, b=b: e.activation(T["junk%d" % b][:], ps(7, 0, 256), AF.Sign, bias=T.kcol[:, b:b + 1], scale=-1.0,
+                                                              accum_out=T[rk][:, b:b + 1]), r=["B7", "kcol%d" % b], w=["junk%d" % b, "%s.%d" % (rk, b)])
+        for b in range(2):
+            ts("onehot%d" % b, T.oh[:, b:512:4], T.place[:], T[rk][:, b:b + 1], None, ALU.is_equal, None, [rk + ".%d" % b] + PL, ["oh%d" % b])
+        quant("qoh", "oh", 0, "oh", 0, 128, ["oh0", "oh1"], ["ohq"])
+        mm("lists", 5, "oh", 0, "nm", 0, 128, ["ohq", "nmq"])
+        ts("offt", T[off][:, 0:1], ps(5, 4, 5), ps(5, 6, 7), None, ALU.add, None, ["B5"], [off + "t"])
+        op("V", "tokq", lambda e: e.tensor_copy(w32(T[win + "q"][:, 0:16]), w32(T.xq[:, 0:256]).indirect(T[off][:, 0:1])), r=["x", off + "t"], w=[win + ".tq"])
+        op("A", "toks", lambda e: e.activation(T[win + "s"][:, 0:16], T.xs[:, 0:256].indirect(T[off][:, 0:1]), AF.Copy), r=["x", off + "t"], w=[win + ".ts"])
+        send("snd_tq", [win + ".tq"], u8(T[win + "q"][:, 0:8]), lambda q: u8(T[win + "q"][:, 16 * slot(r, q):16 * slot(r, q) + 8]), "rt%d" % t)
+        send("snd_ts", [win + ".ts"], T[win + "s"][:, 0:8], lambda q: T[win + "s"][:, 16 * slot(r, q):16 * slot(r, q) + 8], "rt%d" % t)
+        op("X", "arr_t", None, w=["land" + win], ext=(T.sem["rt%d" % t], 2 * lanes * (N - 1)))
+        ts("offc", T[off][:, 2:3], ps(5, 0, 1), ps(5, 2, 3), None, ALU.add, None, ["B5"], [off + "c"])
+        op("V", "candq", lambda e: e.tensor_copy(w32(T[win + "q"][:, 128:144]), w32(T.callq[:, 0:256]).indirect(T[off][:, 2:3])), r=CALL + [off + "c"], w=[win + ".cq"])
+        op("A", "cands", lambda e: e.activation(T[win + "s"][:, 128:144], T.calls[:, 0:256].indirect(T[off][:, 2:3]), AF.Copy), r=CALL + [off + "c"], w=[win + ".cs"])
+        if t + 1 < R:
+            ts("won", T.won[:], T[rk][:], 224.0, -4352.0, ALU.is_gt, ALU.mult, [rk + ".0", rk + ".1"], ["won"])
+            ts("won", T.won[:], T.won[:], 256.0, None, ALU.add, None, ["won"], ["won"])
+            tt("cap", T.cap[:], T.cap[:], T.won[:], ALU.min, ["won", "cap"], ["cap"])
+        else:
+            for s in range(R):
+                for b in range(2):
+                    rs = "rk%d" % s
+                    ts("ohn", T.ohn[:, 64 * s + b:64 * s + 64:4], T.placen[:], T[rs][:, b:b + 1], None, ALU.is_equal, None,
+                       ["ohn", "placen", rs + ".%d" % b], ["ohn%d%d" % (s, b)])
+            quant("qohn", "ohn", 0, "ohn", 0, 128, ["ohn"] + ["ohn%d%d" % (s, b) for s in range(R) for b in range(2)], ["ohnq"])
+            mm("sel0", 6, "nm", 0, "ohn", 0, 128, ["nmq", "ohnq"], True, False)
+            mm("sel1", 6, "nm", 2, "ohn", 0, 128, ["nmq", "ohnq"], False, True)
+            acopy("selrow", T.selrow[0:1, :], T.ps6[0:1, 0:48], ["B6"], ["selrow"])
+            load("S", "st_sel", T.sel[0:1, :], T.selrow[0:1, :], r=["selrow"], w=["out.sel"])
+        if t == 0:
+            for c in range(5):
+                for b in range(2):
+                    acopy("vblk", T.vblk[:, 32 * c + 16 * b:32 * c + 16 * b + 16], T.vrow[:, 16 * c:16 * c + 16],
+                          ["vrow"] + ["vrow.%d" % k for k in range(M)], ["vblk%d%d" % (c, b)])
+            for b in range(4):
+                acopy("eb", T.eb[:, 512 * b + b:512 * b + 512:4], T.ident[:], ["ident"], [EB[b]], scale=0.5)
+            acopy("sq", T.sq[:], ps(0, 128, 256), ["B0"], ["sq"])
+            quant("qzv", "vin", 0, "zt", 0, 128, ["zt"], ["vin.q", "vin.s"])
+            memset("ms_low", T.low[:], -1e29, ["low"])
+            memset("ms_fac", T.fac[:], 0.5, ["fac0", "fac1"])
+            ts("offo", T.offo[:], T.pl[:], 5.0, 4.0, ALU.mult, ALU.add, ["pl"], ["offo"])
+            memset("ms_fac0", T.fac[:, 0:80:5], 0.0, ["fac0"])
+            memset("ms_fac1", T.fac[:, 1:80:5], 1.0, ["fac1"])
+            op("V", "vtr", lambda e: e.transpose(T.vtr[:], T.vblk[:]), r=["vblk%d%d" % (c, b) for c in range(5) for b in range(2)], w=["vtr"])
+            vcopy("offv", T.offv[:, 0:5], T.vtr[:, 0:160:32], ["vtr"], ["offv"])
+            quant("qeb", "eb", 0, "eb", 0, 512, EB, ["ebq"])
+        if t == 1:
+            quant("qw", "w", 0, "wt", 0, 256, ["wt"], ["w"])
+        if t:
+            pick_out(t - 1)
+            products(t - 1)
+        WIN = ["land" + win, win + ".tq", win + ".ts", win + ".cq", win + ".cs", "offv"]
+        op("V", "vinq", lambda e: e.tensor_copy(w32(T.vinq[:, 0:80]), w32(T[win + "q"][:, 0:144]).indirect(T.offv[:, 0:5])), r=WIN, w=["vin.q"])
+        op("A", "vins", lambda e: e.activation(T.vins[:, 0:80], T[win + "s"][:, 0:144].indirect(T.offv[:, 0:5]), AF.Copy), r=WIN, w=["vin.s"])
+        for b in range(4):
+            mm("dec%d" % b, 4 + b, "eb", 128 * b, "vin", 0, 128, ["ebq", "vin.q", "vin.s"])
+        for b in range(4):
+            op("V", "rec%d" % b, lambda e, b=b: e.tensor_tensor_scan(T.h[:, b:4 * NV:4], T.fac[:], ps(4 + b, 0, NV), 0.0, ALU.mult, ALU.add),
+               r=["B%d" % (4 + b), "fac0", "fac1"], w=["h%d" % b])
+        v = "v%d" % t
+        quant("qv", v, 0, "h", 0, 128, HT + ["hu", "hc0", "hc1"], [v])
+        zmul(v)
+
+    for t in range(R):
+        one_round(t)
+
+    n = R * M
+    pick_out(R - 1)
+    marks(R, 0)
+    marks(R, 1)
+    turn(R)
+    load("S", "st_oc", T.oc[:, :], u8(T.voq[:, 0:n]), r=["vo.q%d" % t for t in range(R)], w=["out.oc"])
+    for k in range(4):
+        load("A" if k % 2 else "S", "st_osc%d" % k, T.osc[4 * k:4 * k + 4, :], T.vos[32 * k:32 * k + 4, 0:n], r=["vo.s%d" % t for t in range(R)], w=["out.osc%d" % k])
+    products(R - 1)
+    load("S", "st_y", T.y[:, :], T.yt[:], r=["yt%d%d" % (t, o) for t in range(R) for o in range(O)], w=["out.y"])
+    for a in range(4):
+        load("A" if a % 2 else "S", "st_mk%d" % a, T.mk[0:1, 64 * a:64 * a + 64], T["mt%d" % (R % 2)][32 * a:32 * a + 1, :], r=["mt%d" % (R % 2)], w=["out.mk%d" % a])
+    op("S", "end", None, r=["out.sel", "out.oc", "out.y"] + ["out.osc%d" % k for k in range(4)] + ["out.mk%d" % a for a in range(4)])
+    _emit(P, g, T)
+    g.wait_ge(T.sem.ls, sent[0])

@@ -1,7 +1,9 @@
 from concourse.bass import DstId, RemoteDMATransfer
-from concourse.mybir import dt, AluOpType as ALU, AxisListType, ActivationFunctionType as AF
+from concourse.mybir import dt, AluOpType as ALU, ActivationFunctionType as AF
 
 M, R, O = 16, 3, 2
+HELPERS = 2
+RELAY = {"cq": (), "ca": (), "cb": (), "tq": (), "ts": ()}
 BFT, F32, I32, U16, COD, PLN = "bfloat16", "float32", "int32", "uint16", "float8_e4m3fn_x4", "uint8"
 SCRATCH = {}
 
@@ -15,36 +17,31 @@ def _codes(name, n):
     _sb(name + "s", n, PLN)
 
 
-for _n, _w in (("ctile", 512), ("zt", 512), ("xt", 1024), ("xu", 1024), ("wt", 1024), ("h", 512), ("ind", 512), ("tab", 2048),
-               ("kt", 1024), ("oh", 512), ("ohn", 512), ("nm", 520), ("eb", 2048), ("wgt", 512), ("gmask", 8),
-               ("ones", 128), ("ident", 128), ("place", 128), ("placen", 16), ("sg", 128), ("junk0", 256), ("junk1", 256)):
+for _n, _w in (("ctile", 512), ("zt", 516), ("xt", 1024), ("xu", 1024), ("wt", 1024), ("h", 512), ("ind", 512),
+               ("ones", 128), ("ident", 128), ("sg", 128), ("junk0", 256), ("junk1", 256), ("junk2", 512), ("junk3", 64)):
     _sb(_n, _w, BFT)
-for _n, _w in (("mrow", 256), ("d0", 256), ("d1", 256), ("run0", 256), ("run1", 256), ("kcol", 2), ("cap", 2), ("o16", 2),
-               ("tot", 2), ("md", 3), ("step", 7), ("fac", 80), ("low", 16), ("sq", 128),
-               ("vrow", 80), ("vblk", 160), ("vtr", 160), ("yt", 96), ("selrow", 48), ("name", 2), ("won", 2)):
+for _n, _w in (("mrow", 256), ("d0", 256), ("d1", 256), ("run0", 256), ("run1", 256), ("fac", 80), ("low", 16), ("sq", 128),
+               ("bc", 64), ("mtb", 64), ("v16", 16), ("vrow", 80), ("vblk", 160), ("vtr", 160), ("yt", 96), ("name", 2),
+               ("ks0", 64), ("ks1", 64), ("krow", 256), ("kinit", 2), ("num", 2), ("rk", 4), ("won", 2), ("selc", R),
+               ("placet", 32), ("placec", 32), ("rest", 64), ("hit", 64), ("hitt", 64), ("pair", 64), ("part", 1)):
     _sb(_n, _w, F32)
-for _t in range(R):
-    _sb("rk%d" % _t, 2, F32)
 for _t in range(2):
     _sb("mk%d" % _t, 96, F32)
     _sb("mt%d" % _t, 64, F32)
-for _n, _w in (("pn", 2), ("pl", 2), ("ph", 2), ("vi", 80), ("vi2", 80), ("v16", 16)):
+for _n, _w in (("pn", 2), ("pl", 2), ("vi", 80), ("vi2", 80)):
     _sb(_n, _w, I32)
 _sb("offv", 6, U16)
-_sb("offk", 16, U16)
 _sb("offo", 2, U16)
 for _t in range(R):
     _sb("off%d" % _t, 4, U16)
-    _sb("cnt%d" % _t, 2, BFT)
-    _sb("land%d" % _t, 14, BFT)
+    _sb("land%d" % _t, 80, BFT)
     _codes("win%d" % _t, 144)
     _codes("v%d" % _t, 128)
-for _n, _w in (("c", 128), ("call", 256), ("x", 256), ("xu", 256), ("w", 256), ("vu", 128), ("vo", 48), ("ind", 128), ("kt", 256),
-               ("oh", 128), ("ohn", 128), ("nm", 130), ("eb", 512), ("wgt", 128), ("vin", 128)):
+for _n, _w in (("c", 128), ("call", 256), ("x", 256), ("xu", 256), ("w", 256), ("vu", 128), ("vo", 48), ("ind", 128), ("eb", 512), ("vin", 128)):
     _codes(_n, _w)
 for _b in range(8):
     SCRATCH["ps%d" % _b] = ("psum", [128, 512], F32)
-SEMAPHORES = ["rc"] + ["rn%d" % t for t in range(R)] + ["rt%d" % t for t in range(R)] + ["ls"] + ["e%d" % i for i in range(140)]
+SEMAPHORES = ["rc", "ra", "rb"] + ["r%s%d" % (k, t) for k in "nqs" for t in range(R)] + ["ls"] + ["e%d" % i for i in range(130)]
 
 
 def _add(P, q, name, fn, r=(), w=(), inc=1, ext=None):
@@ -118,52 +115,126 @@ def _emit(P, g, T):
             val[i] = (s["sem"], s["n"])
 
 
-def rank_program(g, core, T, topo):
-    r = T.rank_of(core)
-    if r is None:
-        return
-    cores = list(T.cores)
-    N = len(cores)
-    P = {"ops": [], "tags": {}}
+def _count(mask):
+    return bin(mask).count("1")
+
+
+def _ways(cores, r, topo):
     chip = [topo.chip(q) for q in cores]
     ways = {"far": [], "plane": [], "mate": []}
-    for d in range(1, N):
+    for d in range(1, len(cores)):
         q = r ^ d
         way = "mate" if topo.mates(chip[r], chip[q]) else "plane" if topo.same_plane(chip[r], chip[q]) else "far"
         ways[way].append(q)
+    plane = list(ways["plane"])
     others = []
     while ways["far"] or ways["plane"]:
         for way in ("far", "plane"):
             others += ways[way][:1]
             del ways[way][:1]
     others += ways["mate"]
-    mask = 0xFFFF
+    me = cores[r]
+    helpers = [c for c in topo.cores_of(me) if c not in cores and topo.die(c) == topo.die(me)
+               and all(topo.may_write(c, cores[q]) for q in plane)][:HELPERS]
+    far = near = -1
     for q in others:
-        mask &= topo.mask(core, cores[q])
-    lanes = len([e for e in topo.engines(core, cores[others[0]]) if mask >> e & 1])
+        far &= topo.mask(me, cores[q])
+    for c in helpers:
+        near &= topo.mask(me, c)
+    return others, plane, helpers, far, near & ~far
+
+
+def _dst(topo, c):
+    rid, pid, _ = topo.addr(c)
+    return DstId(rid=rid, pnc=pid)
+
+
+def _u8(ap):
+    return ap.bitcast(dt.uint8)
+
+
+def _slot(src, dst, n):
+    return (src - dst) % n
+
+
+def _pieces(T, r, others, plane):
+    n = len(others) + 1
+    half = [q for q in others if 2 * q // n == 2 * r // n]
+    raw = [("cq", _u8(T.cq[:, 0:32]), lambda q: _u8(T.callq[:, 32 * r:32 * r + 32]), "rc", others),
+           ("ca", T.cs[:, 0:32], lambda q: T.calls[:, 32 * r:32 * r + 32], "ra", [q for q in others if q not in half]),
+           ("cb", T.cs[:, 0:32], lambda q: T.calls[:, 32 * r:32 * r + 32], "rb", half)]
+    for t in range(R):
+        wq, ws = T["win%dq" % t], T["win%ds" % t]
+        raw.append(("tq", _u8(wq[:, 0:8]), lambda q, w=wq: _u8(w[:, 16 * _slot(r, q, n):16 * _slot(r, q, n) + 8]), "rq%d" % t, others))
+        raw.append(("ts", ws[:, 0:8], lambda q, w=ws: w[:, 16 * _slot(r, q, n):16 * _slot(r, q, n) + 8], "rs%d" % t, others))
+    out = []
+    for kind, src, dst, sem, to in raw:
+        free, shares = [q for q in plane if q in to], []
+        for k in RELAY[kind]:
+            shares.append(free[:k])
+            del free[:k]
+        out.append((src, dst, sem, [q for q in to if not any(q in s for s in shares)], shares))
+    return out
+
+
+def _helper(g, core, T, topo, cores, r):
+    others, plane, helpers, far, near = _ways(cores, r, topo)
+    j = helpers.index(core)
+    sent = 0
+    for src, dst, sem, direct, shares in _pieces(T, r, others, plane):
+        share = shares[j] if j < len(shares) else []
+        if not share:
+            continue
+        mask = far
+        for q in share:
+            mask &= topo.mask(core, cores[q])
+        g.wait_ge(T.sem[sem], _count(near))
+        g.remote_dma_fused([RemoteDMATransfer(dst_ids=[_dst(topo, cores[q]) for q in share], dma_engine_mask=mask, remote_sem=T.sem[sem],
+                                              srcs=[src], dsts=[dst(q) for q in share])], local_sem=T.sem.ls)
+        sent += _count(mask)
+    if sent:
+        g.wait_ge(T.sem.ls, sent)
+
+
+def rank_program(g, core, T, topo):
+    cores = list(T.cores)
+    N = len(cores)
+    r = T.rank_of(core)
+    if r is None:
+        for q in range(N):
+            if core in _ways(cores, q, topo)[2]:
+                _helper(g, core, T, topo, cores, q)
+        return
+    P = {"ops": [], "tags": {}}
+    others, plane, helpers, mask, near = _ways(cores, r, topo)
+    lanes = _count(mask)
     sent = [0]
+    piece = _pieces(T, r, others, plane)
 
     def op(*a, **k):
         _add(P, *a, **k)
 
-    def u8(ap):
-        return ap.bitcast(dt.uint8)
+    u8 = _u8
 
     def w32(ap):
         return ap.bitcast(dt.uint32)
 
     def slot(src, dst):
-        return (src - dst) % N
+        return _slot(src, dst, N)
 
-    def send(name, reads, src, dst, sem):
-        ids = []
-        for q in others:
-            rid, pid, _ = topo.addr(cores[q])
-            ids.append(DstId(rid=rid, pnc=pid))
-        dsts = [dst(q) for q in others]
+    def send(name, reads, src, dst, sem, direct, shares=()):
+        tr = [RemoteDMATransfer(dst_ids=[_dst(topo, cores[q]) for q in direct], dma_engine_mask=mask, remote_sem=T.sem[sem],
+                                srcs=[src], dsts=[dst(q) for q in direct])]
         sent[0] += lanes
-        op("G", name, lambda e: e.remote_dma_fused([RemoteDMATransfer(dst_ids=ids, dma_engine_mask=mask, remote_sem=T.sem[sem],
-                                                                      srcs=[src], dsts=dsts)], local_sem=T.sem.ls), r=reads)
+        via = [c for c, s in zip(helpers, shares) if s]
+        if via:
+            tr.append(RemoteDMATransfer(dst_ids=[_dst(topo, c) for c in via], dma_engine_mask=near, remote_sem=T.sem[sem],
+                                        srcs=[src], dsts=[src for c in via]))
+            sent[0] += _count(near)
+        op("G", name, lambda e: e.remote_dma_fused(tr, local_sem=T.sem.ls), r=reads)
+
+    def arrive(tag, sem, senders):
+        op("X", "arr", None, w=[tag], ext=(T.sem[sem], lanes * senders))
 
     def memset(name, ap, v, w):
         op("V", name, lambda e: e.memset(ap, v), w=w)
@@ -187,77 +258,92 @@ def rank_program(g, core, T, topo):
     def tt(name, out, in0, in1, o, r, w):
         op("V", name, lambda e: e.tensor_tensor(out, in0, in1, o), r=r, w=w)
 
+    def scan(name, out, d0, d1, first, o0, o1, r, w):
+        op("V", name, lambda e: e.tensor_tensor_scan(out, d0, d1, first, o0, o1), r=r, w=w)
+
+    def flip(name, out, in_, r, w):
+        op("V", name, lambda e: e.transpose(out, in_), r=r, w=w)
+
     def vcopy(name, out, in_, r, w):
         op("V", name, lambda e: e.tensor_copy(out, in_), r=r, w=w)
 
     def acopy(name, out, in_, r, w, **k):
         op("A", name, lambda e: e.activation(out, in_, AF.Copy, **k), r=r, w=w)
 
+    def ramp(name, out, n, first, step, r, w):
+        op("A", name, lambda e: e.activation(out, T.v16[:, 0:n], AF.Identity, bias=float(first), scale=float(step)), r=["v16"] + r, w=w)
+
     def load(q, name, out, in_, r=(), w=()):
         op(q, name, lambda e: e.dma_start(out, in_), r=r, w=w, inc=16)
+
+    def runs(v):
+        cuts = [0] + [k for k in range(1, len(v)) if v[k] != v[k - 1] - 1] + [len(v)]
+        return list(zip(cuts, cuts[1:]))
 
     order = [None] * M
     for k in range(M):
         i, h = (r - k) % N, k // N
         order[(i % 4) + 4 * h + 8 * (i // 4)] = k
-    place_of = {k: j for j, k in enumerate(order)}
     HT = ["h0", "h1", "h2", "h3"]
     EB = ["eb0", "eb1", "eb2", "eb3"]
-    PL = ["place%d" % j for j in range(M)]
-    RND = 1.5 * 2.0 ** 27
+    VIN = ["vin.q0", "vin.q2", "vin.s0", "vin.s2"]
     CV = 96
     NV = 5 * M
+    OWN = 2 * N
+    HB = 2 * r // N
+    ALL = R * M
 
     load("S", "ldc", T.ctile[:, 0:128], T.c[:, :], w=["ctile"])
-    load("A", "ldx", T.xt[:, :], T.x[:, :], w=["xt"])
+    load("S", "ldx", T.xt[:, :], T.x[:, :], w=["xt"])
     memset("ms_c", T.ctile[:, 128:512], 0.0, ["ctile0"])
     memset("ms_ones", T.ones[:], 1.0, ["ones"])
     memset("ms_h", T.h[:], 0.0, HT + ["hu", "hc0", "hc1"])
-    memset("ms_h1", T.h[:, 4 * CV:4 * CV + 2], 1.0, ["hc0"])
-    memset("ms_h2", T.h[:, 4 * CV + 6:4 * CV + 8], 1.0, ["hc1"])
     load("S", "ldu", T.h[:, 4 * NV:4 * NV + 4], T.u[:, 0:4], w=["hu"])
-    memset("ms_zt", T.zt[:], 0.0, ["zt"])
     op("G", "pn", lambda e: e.iota(T.pn[:], [[128, 2]], 0, 1), w=["pn"])
+    op("G", "v16", lambda e: e.iota(T.v16[:], [[1, 16]], 0, 0, allow_small_or_imprecise_dtypes=True), w=["v16"])
     op("G", "vi", lambda e: e.iota(T.vi[:], [[4, 2], [16, 8], [17, 5]], 256 - 17 - 16 * r, 0), w=["vi"])
-    op("G", "v16", lambda e: e.iota(T.v16[:], [[1, 16]], 0, 0), w=["v16"])
-    op("G", "ident", lambda e: e.affine_select(T.ident[:], T.ones[:], [[-1, 128]], ALU.is_equal, 0.0, 0, 1), r=["ones"], w=["ident"])
 
     quant("qc", "c", 0, "ctile", 0, 128, ["ctile", "ctile0"], ["c"])
-    send("snd_cq", ["c"], u8(T.cq[:, 0:32]), lambda q: u8(T.callq[:, 32 * r:32 * r + 32]), "rc")
-    send("snd_cs", ["c"], T.cs[:, 0:32], lambda q: T.calls[:, 32 * r:32 * r + 32], "rc")
+    for j in range(3):
+        send("snd_c", ["c"], *piece[j])
     load("S", "ownq", u8(T.callq[:, 32 * r:32 * r + 32]), u8(T.cq[:, 0:32]), r=["c"], w=["own.q"])
     load("S", "owns", T.calls[:, 32 * r:32 * r + 32], T.cs[:, 0:32], r=["c"], w=["own.s"])
-    op("X", "arr_c", None, w=["call"], ext=(T.sem.rc, 2 * lanes * (N - 1)))
-    CALL = ["call", "own.q", "own.s"]
+    arrive("call.q", "rc", N - 1)
+    arrive("call.a", "ra", N // 2)
+    arrive("call.b", "rb", N // 2 - 1)
+    CALL = ["call.q", "call.a", "call.b", "own.q", "own.s"]
 
-    for j in range(M):
-        acopy("place", T.place[:, j:128:16], T.ones[:, 0:8], ["ones"], [PL[j]], scale=255.0 - 2.0 * order[j])
-    memset("ms_kt", T.kt[:], 0.0, ["kta", "ktb", "kto0", "kto1", "ktr0", "ktr1", "ktc", "ktd"])
-    for t in range(2):
-        memset("ms_mk%d" % t, T["mk%d" % t][:, 32:96], 0.0, ["mk%d.0" % t, "mk%d.1" % t])
+    PT, PC = [], ["placec0", "placec1"]
+    for a, b in runs(order):
+        PT.append("placet%d" % a)
+        ramp("place", T.placet[:, a:b], b - a, 255 - 2 * order[a], 2, [], PT[-1:])
+    for j in range(2):
+        ramp("place", T.placec[:, M * j:M * j + M], M, 255, -2, [], [PC[j]])
+    acopy("place", T.placet[:, M:2 * M], T.placet[:, 0:M], list(PT), ["placet."])
+    PT.append("placet.")
+    op("G", "ident", lambda e: e.affine_select(T.ident[:], T.ones[:], [[-1, 128]], ALU.is_equal, 0.0, 0, 1), r=["ones"], w=["ident"])
+    memset("ms_h1", T.h[:, 4 * CV:4 * CV + 2], 1.0, ["hc0"])
+    memset("ms_h2", T.h[:, 4 * CV + 6:4 * CV + 8], 1.0, ["hc1"])
+    memset("ms_zt", T.zt[:], 0.0, ["zt"])
+    memset("ms_mk0", T.mk0[:, 32:96], 0.0, ["mk0.0", "mk0.1"])
+    memset("ms_mk1", T.mk1[:, 32:96], 0.0, ["mk1.0", "mk1.1"])
+    quant("qzv", "vin", 0, "zt", 0, 128, ["zt"], VIN)
+    acopy("eb", T.zt[:, 3:515:4], T.ident[:], ["ident"], ["zt"], scale=0.5)
+    ts("vi2", T.vi2[:], T.vi[:], 127, None, ALU.bitwise_and, None, ["vi"], ["vi2"])
+    ts("pl", T.pl[:], T.pn[:], 15, None, ALU.bitwise_and, None, ["pn"], ["pl"])
+    vcopy("vrow", T.vrow[:], T.vi2[:], ["vi2"], ["vrow"])
+    vcopy("num", T.num[:], T.pn[:], ["pn"], ["num"])
+    memset("ms_land", T.land0[:, OWN:], 0.0, ["cnt0"])
+    ramp("vrowk", T.vrow[:, 0:NV:5], M, 128, 1, ["vrow"], ["vrow"])
     for a in range(4):
         for b in range(2):
             (vcopy if b else acopy)("xu", T.xu[:, 512 * b + 128 * a:512 * b + 128 * a + 128], T.xt[:, 256 * a + 128 * b:256 * a + 128 * b + 128],
                                     ["xt"], ["xu%d%d" % (a, b)])
     quant("qv", "vu", 0, "h", 0, 128, HT + ["hu", "hc0", "hc1"], ["vu"])
     quant("qxu", "xu", 0, "xu", 0, 256, ["xu%d%d" % (a, b) for a in range(4) for b in range(2)], ["xuq"])
-    acopy("z_nm", T.nm[:, 0:512], T.zt[:], ["zt"], ["nm", "nmlo", "nmhi"])
-    acopy("z_oh", T.oh[:], T.zt[:], ["zt"], ["oh0", "oh1"])
-    ts("pl", T.pl[:], T.pn[:], 15, None, ALU.bitwise_and, None, ["pn"], ["pl"])
-    ts("vi2", T.vi2[:], T.vi[:], 127, None, ALU.bitwise_and, None, ["vi"], ["vi2"])
-    for d in range(3):
-        ts("md", T.md[:, d:d + 1], T.pl[:, 0:1], 3.0 + d, None, ALU.is_equal, None, ["pl"], ["md%d" % d])
-    vcopy("vrow", T.vrow[:], T.vi2[:], ["vi2"], ["vrow"])
-    for k in range(7):
-        acopy("step", T.step[:, k:k + 1], T.md[:, 1 + k // 4:2 + k // 4], ["md%d" % (1 + k // 4)], ["step%d" % k], scale=16.0 * 2 ** k)
-    quant("qx", "x", 0, "xt", 0, 256, ["xt"], ["x"])
-    memset("ms_wgt", T.wgt[:], 256.0, ["wgt"])
-    memset("ms_wgt", T.wgt[:, 2:512:4], 1.0, ["wgt"])
-    op("G", "ktc", lambda e: e.iota(T.kt[32:33, 2:1024:4], [[0, 16], [-1, 16]], 15, 0, allow_small_or_imprecise_dtypes=True), w=["ktc", "ktc2"])
-    op("G", "ktd", lambda e: e.iota(T.kt[64:65, 2:1024:4], [[-16, 16], [0, 16]], 240, 0, allow_small_or_imprecise_dtypes=True),
-       w=["ktd", "ktd2", "ktd3"])
-    op("G", "gmask0", lambda e: e.affine_select(T.gmask[:], T.ones[:, 0:8], [[-16, 8]], ALU.is_ge, 0.0, 0, 1), r=["ones"], w=["gmask"])
-    op("G", "gmask1", lambda e: e.affine_select(T.gmask[:], T.gmask[:], [[16, 8]], ALU.is_ge, 0.0, 15, -1), r=["gmask"], w=["gmask"])
+    for c in range(5):
+        for b in range(2):
+            acopy("vblk", T.vblk[:, 32 * c + 16 * b:32 * c + 16 * b + 16], T.vrow[:, 16 * c:16 * c + 16], ["vrow"], ["vblk%d%d" % (c, b)])
 
     def zmul(v):
         for b in range(2):
@@ -271,46 +357,47 @@ def rank_program(g, core, T, topo):
         if t == 0:
             vcopy("mark%d" % b, mk(0, b), ps(4 + b, NV, NV + 1), ["B%d" % (4 + b)], [q])
         else:
-            op("V", "mark%d" % b, lambda e: e.tensor_tensor_scan(T["mk%d" % (t % 2)][:, 32 * b + 33 - M:32 * b + 33], T["ps%d" % (4 + b)][:, 4:NV:5],
-                                                                 T.low[:], mk(t - 1, b), ALU.max, ALU.max),
-               r=["B%d" % (4 + b), "low", "mk%d.%d" % ((t - 1) % 2, b)], w=[q])
+            scan("mark%d" % b, T["mk%d" % (t % 2)][:, 32 * b + 33 - M:32 * b + 33], T["ps%d" % (4 + b)][:, 4:NV:5], T.low[:], mk(t - 1, b),
+                 ALU.max, ALU.max, ["B%d" % (4 + b), "low", "mk%d.%d" % ((t - 1) % 2, b)], [q])
 
     def turn(t):
-        op("V", "turn", lambda e: e.transpose(T["mt%d" % (t % 2)][:], T["mk%d" % (t % 2)][:, 32:96]),
-           r=["mk%d.0" % (t % 2), "mk%d.1" % (t % 2)], w=["mt%d" % (t % 2)])
+        flip("turn", T["mt%d" % (t % 2)][:], T["mk%d" % (t % 2)][:, 32:96], ["mk%d.0" % (t % 2), "mk%d.1" % (t % 2)], ["mt%d" % (t % 2)])
 
     def spread(t, aa):
         for a in aa:
             op("G", "spread%d" % a, lambda e, a=a: e.partition_broadcast(T.mrow[:, 64 * a:64 * a + 64], T["mt%d" % (t % 2)][32 * a:32 * a + 1, :], 128),
-               r=["mt%d" % (t % 2)], w=["mrow%d" % a])
+               r=["mt%d" % (t % 2)], w=["mrow%d.%d" % (a, q) for q in range(4)])
+
+    def widen(t):
+        for b in range(2):
+            acopy("bc", T.bc[:, 32 * b:32 * b + 32], T.ones[:, 0:32], ["ones", "mk%d.%d" % (t % 2, b)], ["bc%d" % b], scale=mk(t, b))
+
+    def spread_a(aa):
+        for a in aa:
+            for q in range(4):
+                acopy("spa", T.mrow[32 * q:32 * q + 32, 64 * a:64 * a + 64], T.mtb[32 * a:32 * a + 32, :], ["mtb"], ["mrow%d.%d" % (a, q)])
 
     zmul("vu")
+    quant("qx", "x", 0, "xt", 0, 256, ["xt"], ["x"])
     marks(0, 0)
     marks(0, 1)
-    quant("qwgt", "wgt", 0, "wgt", 0, 128, ["wgt"], ["wgtq"])
+    ts("kinit", T.kinit[:], T.num[:], -1.0 / 256, 255.0 / 256, ALU.mult, ALU.add, ["num"], ["kinit"])
     turn(0)
     spread(0, (0, 1, 2, 3))
-    ts("tab", T.tab[:, 0:16], T.v16[:], T.md[:, 0:1], None, ALU.mult, None, ["v16", "md0"], ["tab0"])
-    memset("ms_cap", T.cap[:], 256.0, ["cap"])
-    for k in range(5):
-        m = 16 << k
-        ts("tab", T.tab[:, m:2 * m], T.tab[:, 0:m], T.step[:, k:k + 1], None, ALU.add, None, ["tab%d" % j for j in range(k + 1)] + ["step%d" % k], ["tab%d" % (k + 1)])
-    TOP = 256 * (N - 1) + 16
-    TAB = ["tab%d" % j for j in range(8)]
-    memset("kt32", T.kt[32:33, 130:1024:512], 0.0, ["ktc"])
-    memset("kt96", T.kt[96:97, 130:1024:512], 15.0, ["ktc2"])
-    memset("kt64", T.kt[64:65, 258:1024:512], 0.0, ["ktd"])
-    memset("kt96", T.kt[96:97, 258:259], 176.0, ["ktd2"])
-    memset("kt96", T.kt[96:97, 770:771], 48.0, ["ktd3"])
-    for k in range(M):
-        acopy("vrowk", T.vrow[:, 5 * k:5 * k + 1], T.ones[:, 0:1], ["vrow", "ones"], ["vrow.%d" % k], scale=float(128 + place_of[k]))
-    for k in (5, 6):
-        op("A", "tab", lambda e, m=16 << k, k=k: e.activation(T.tab[:, m:min(2 * m, TOP)], T.tab[:, 0:min(m, TOP - m)], AF.Identity, bias=T.step[:, k:k + 1]),
-           r=["tab%d" % j for j in range(k + 1)] + ["step%d" % k], w=["tab%d" % (k + 1)])
+    memset("ms_low", T.low[:], -1e29, ["low"])
+    memset("ms_fac", T.fac[:], 0.5, ["fac0", "fac1"])
+    ts("offo", T.offo[:], T.pl[:], 5.0, 4.0, ALU.mult, ALU.add, ["pl"], ["offo"])
+    memset("ms_fac0", T.fac[:, 0:80:5], 0.0, ["fac0"])
+    memset("ms_fac1", T.fac[:, 1:80:5], 1.0, ["fac1"])
+    flip("vtr", T.vtr[:], T.vblk[:], ["vblk%d%d" % (c, b) for c in range(5) for b in range(2)], ["vtr"])
+    quant("qeb", "eb", 0, "zt", 3, 128, ["zt"], [EB[0]])
+    vcopy("offv", T.offv[:, 0:5], T.vtr[:, 0:160:32], ["vtr"], ["offv"])
+    for b in range(1, 4):
+        quant("qeb", "eb", 128 * b, "zt", 3 - b, 128, ["zt"], [EB[b]])
 
-    def above(t, b, k):
-        ts("above", T.ind[:, 2 * k + b:512:4], ps(b, 128 * k, 128 * k + 128), mk(t, b), None, ALU.is_gt, None,
-           ["B%d" % b, "mk%d.%d" % (t % 2, b)], ["ind%d%d" % (b, k)])
+    def above(t, b, k, bank, a):
+        ts("above", T.ind[:, 2 * k + b:512:4], ps(bank, a, a + 128), mk(t, b), None, ALU.is_gt, None,
+           ["B%d" % bank, "mk%d.%d" % (t % 2, b)], ["ind%d%d" % (b, k)])
 
     def above_a(t):
         op("A", "sgn", lambda e: e.activation(T.sg[:], T.sq[:], AF.Sign, bias=mk(t, 0), scale=-1.0), r=["sq", "mk%d.0" % (t % 2)], w=["sg"])
@@ -321,12 +408,11 @@ def rank_program(g, core, T, topo):
 
     def name_diff(b, lo, hi):
         tt("diff%d" % b, T["d%d" % b][:, lo:hi], ps(2 + b, lo, hi), T.mrow[:, lo:hi], ALU.subtract,
-           ["B%d" % (2 + b)] + ["mrow%d" % a for a in range(lo // 64, hi // 64)], pieces("d", b, lo, hi))
+           ["B%d" % (2 + b)] + ["mrow%d.%d" % (a, q) for a in range(lo // 64, hi // 64) for q in range(4)], pieces("d", b, lo, hi))
 
     def name_run(b, lo, hi):
-        first = T["run%d" % b][:, lo - 1:lo] if lo else -1e29
-        op("V", "run%d" % b, lambda e: e.tensor_tensor_scan(T["run%d" % b][:, lo:hi], T["d%d" % b][:, lo:hi], T["d%d" % b][:, lo:hi], first, ALU.max, ALU.max),
-           r=pieces("d", b, lo, hi) + (pieces("run", b, 0, lo) if lo else []), w=pieces("run", b, lo, hi))
+        scan("run%d" % b, T["run%d" % b][:, lo:hi], T["d%d" % b][:, lo:hi], T["d%d" % b][:, lo:hi], T["run%d" % b][:, lo - 1:lo] if lo else -1e29,
+             ALU.max, ALU.max, pieces("d", b, lo, hi) + (pieces("run", b, 0, lo) if lo else []), pieces("run", b, lo, hi))
 
     def name_at(b):
         op("A", "name%d" % b, lambda e: e.activation(T["junk%d" % b][:], T["run%d" % b][:], AF.Sign, bias=T["run%d" % b][:, 255:256], scale=-1.0,
@@ -341,142 +427,144 @@ def rank_program(g, core, T, topo):
         v = "v%d" % t
         for o in range(O):
             mm("y%d" % o, 6 + o, "w", 128 * o, v, 0, 128, ["w", v])
+
+    def product_copies(t):
         for o in range(O):
-            (vcopy if o else acopy)("yc%d" % o, T.yt[:, R * M * o + M * t:R * M * o + M * t + M], T["ps%d" % (6 + o)][:, 4:NV:5],
-                                    ["B%d" % (6 + o)], ["yt%d%d" % (t, o)])
+            acopy("yc%d" % o, T.yt[:, ALL * o + M * t:ALL * o + M * t + M], T["ps%d" % (6 + o)][:, 4:NV:5], ["B%d" % (6 + o)], ["yt%d%d" % (t, o)])
+
+    def rank(b, h):
+        j = 2 * h + b
+        op("A", "rank", lambda e: e.activation(T.junk2[:, 128 * j:128 * j + 128], T.krow[:, 128 * h:128 * h + 128], AF.Sign, bias=T["ks%d" % b][:, 63:64],
+                                               scale=-1.0, accum_out=T.rk[:, j:j + 1]),
+           r=["ks%d" % b] + (["far0", "far1"] if h else ["row0", "row1"] + ["next%d" % q for q in range(4)]), w=["junk2.%d" % j, "rk%d" % j])
+
+    def rests(place, tags):
+        for b in range(2):
+            ts("rest", T.rest[:, 32 * b:32 * b + 32], place[:], T.rk[:, b:b + 1], None, ALU.subtract, None, tags + ["rk%d" % b], ["rest%d" % b])
+
+    def hits(value, tags):
+        for b in range(2):
+            ts("hit", T.hit[:, 32 * b:32 * b + 32], T.rest[:, 32 * b:32 * b + 32], T.rk[:, 2 + b:3 + b], value[:, b:b + 1], ALU.is_equal, ALU.mult,
+               ["rest%d" % b, "rk%d" % (2 + b), tags[b]], ["hit%d" % b])
+        flip("hitt", T.hitt[:], T.hit[:], ["hit0", "hit1"], ["hitt"])
+
+    def sums():
+        op("A", "part", lambda e: e.activation(T.junk3[:], T.hitt[:], AF.Copy, accum_out=T.part[:]), r=["hitt"], w=["junk3", "part"])
+        for q in range(2):
+            a = 32 * (1 - q)
+            scan("pair", T.pair[32 * q:32 * q + 32, :], T.hitt[a:a + 32, :], T.hitt[a + 64:a + 96, :], 0.0, ALU.add, ALU.add, ["hitt"], ["pair%d" % q])
+
+    def total(name, out, w):
+        ts(name, out, T.part[0:64, :], T.part[64:128, :], T.pair[0:64, 63:64], ALU.add, ALU.add, ["part", "pair0", "pair1"], w)
 
     def one_round(t):
-        win, off, rk, cnt, land = "win%d" % t, "off%d" % t, "rk%d" % t, "cnt%d" % t, "land%d" % t
+        win, off, cnt, land = "win%d" % t, "off%d" % t, "cnt%d" % t, "land%d" % t
         if t == 0:
             for b in range(2):
-                mm("sb%d" % b, b, "xu", 128 * b, "call", 0, 256, ["xuq"] + CALL)
+                mm("sb", 4 + b, "xu", 128 * b, "call", 128 * (1 - HB), 128, ["xuq", "call.q", "call.a"])
             for b in range(2):
-                for k in range(2):
-                    above(t, b, k)
+                above(t, b, 1 - HB, 4 + b, 0)
+            for b in range(2):
+                mm("sb", b, "xu", 128 * b, "call", 128 * HB, 128, ["xuq"] + CALL)
+            for b in range(2):
+                above(t, b, HB, b, 0)
         else:
             marks(t, 0)
             above_a(t)
-            above(t, 0, 0)
             marks(t, 1)
+            above(t, 0, 0, 0, 0)
+            above(t, 1, 0, 1, 0)
+            above(t, 1, 1, 1, 128)
             turn(t)
-            above(t, 1, 0)
-            above(t, 1, 1)
+            widen(t)
         quant("qind", "ind", 0, "ind", 0, 128, ["ind00", "ind01", "ind10", "ind11"], ["indq"])
         if t:
-            spread(t, (0, 1))
+            spread(t, (0,))
+            flip("turnw", T.mtb[:], T.bc[:], ["bc0", "bc1"], ["mtb"])
+            spread_a((1, 2, 3))
         mm("cnt", 6, "ind", 0, "vu", 0, 128, ["indq", "vu"])
-        vcopy("cnt", T[cnt][:], ps(6, CV, CV + 2), ["B6"], [cnt])
-        send("snd_n", [cnt], T[cnt][:], lambda q: T[land][:, 2 * slot(r, q) - 2:2 * slot(r, q)], "rn%d" % t)
-        op("X", "arr_n", None, w=[land], ext=(T.sem["rn%d" % t], lanes * (N - 1)))
-        ts("c16", T.o16[:], ps(6, CV, CV + 2), RND, RND, ALU.add, ALU.subtract, ["B6"], ["o16"])
-        tt("crest", T.won[:], ps(6, CV, CV + 2), T.o16[:], ALU.subtract, ["B6", "o16"], ["won"])
-        tt("ccap", T.o16[:], T.o16[:], T.cap[:], ALU.min, ["cap", "o16"], ["o16"])
-        for b in range(2):
-            acopy("own", T.kt[:, 512 * b + 3:512 * b + 512:4], T.ident[:], ["ident", "won"], ["ktr%d" % b], scale=T.won[:, b:b + 1])
-            acopy("own", T.kt[:, 512 * b + 1:512 * b + 512:4], T.ident[:], ["ident", "o16"], ["kto%d" % b], scale=T.o16[:, b:b + 1])
-        if t:
-            spread(t, (2, 3))
-        else:
-            op("G", "placen", lambda e: e.iota(T.placen[:], [[-2, 16]], 255, 0, allow_small_or_imprecise_dtypes=True), w=["placen"])
+        vcopy("cnt", T[land][:, OWN:OWN + 2], ps(6, CV, CV + 2), ["B6"], [cnt])
+        send("snd_n", [cnt], T[land][:, OWN:OWN + 2], lambda q: T[land][:, 2 * slot(r, q):2 * slot(r, q) + 2], "rn%d" % t, others)
+        arrive(land, "rn%d" % t, N - 1)
+        if t == 0:
             for b in range(2):
                 mm("sa%d" % b, 2 + b, "call", 128 * b, "x", 0, 256, ["x"] + CALL)
-        for lo, hi in (((0, 128), (128, 192), (192, 256)) if t else ((0, 256),)):
+            for b in range(2):
+                mm("sb%d" % b, b, "xu", 128 * b, "call", 0, 256, ["xuq"] + CALL)
+            acopy("sq", T.sq[:], ps(0, 128, 256), ["B0"], ["sq"])
+        for lo, hi in (((0, 128), (128, 256)) if t else ((0, 256),)):
             for b in range(2):
                 name_diff(b, lo, hi)
             for b in range(2):
                 name_run(b, lo, hi)
         name_at(0)
-        if t == 0:
-            for b in range(4):
-                load("S", "z_eb", T.eb[:, 512 * b:512 * b + 512], T.zt[:], r=["zt", land], w=[EB[b]])
-        if t == 1:
-            load("S", "ldw", T.wt[:, :], T.w[:, :], r=[land], w=["wt"])
-            load("S", "z_ohn", T.ohn[:], T.zt[:], r=["zt", land], w=["ohn"])
-        for b in range(2):
-            op("V", "tot", lambda e, b=b: e.tensor_reduce(T.tot[:, b:b + 1], T[land][:, b:14:2], AxisListType.X, ALU.add), r=[land], w=["tot%d" % b])
-        for b in range(2):
-            ts("offk", T.offk[:, 8 * b:8 * b + 8], T.gmask[:], T.tot[:, b:b + 1], None, ALU.mult, None, ["gmask", "tot%d" % b], ["offk%d" % b])
-        op("A", "gain1", lambda e: e.activation(T.kt[:, 512:1024:4], T.tab[:, 0:TOP].indirect(T.offk[:, 8:16]), AF.Copy), r=TAB + ["offk1"], w=["ktb"])
-        op("V", "gain0", lambda e: e.tensor_copy(T.kt[:, 0:512:4], T.tab[:, 0:TOP].indirect(T.offk[:, 0:8])), r=TAB + ["offk0"], w=["kta"])
         name_at(1)
-        KC = ["ktc", "ktd", "ktc2", "ktd2", "ktd3"]
-        quant("qkta", "kt", 0, "kt", 0, 128, ["kta", "kto0", "ktr0"] + KC, ["ktqa"])
-        quant("qktb", "kt", 128, "kt", 512, 128, ["ktb", "kto1", "ktr1"] + KC, ["ktqb"])
-        mm("kcol0", 6, "kt", 0, "wgt", 0, 128, ["ktqa", "wgtq"])
-        mm("krow", 7, "wgt", 0, "kt", 0, 256, ["ktqa", "ktqb", "wgtq"])
-        mm("kcol1", 4, "kt", 128, "wgt", 0, 128, ["ktqb", "wgtq"])
-        if t == 0:
-            ts("ph", T.ph[:], T.pn[:], 240, None, ALU.bitwise_and, None, ["pn"], ["ph"])
-            vcopy("nm_l", T.nm[:, 0:2], T.pl[:], ["pl", "nm"], ["nm_l"])
-        vcopy("kcc0", T.kcol[:, 0:1], ps(6, 0, 1), ["B6"], ["kcol0"])
-        if t == 0:
-            vcopy("nm_h", T.nm[:, 8:10], T.ph[:], ["ph", "nm"], ["nm_h"])
-            memset("z_nm2", T.nm[:, 512:520], 0.0, ["nm2"])
-        ts("n16", T.nm[:, 24:26], T.name[:], RND, RND, ALU.add, ALU.subtract, ["name0", "name1", "nm"], ["nmhi"])
-        vcopy("kcc1", T.kcol[:, 1:2], ps(4, 0, 1), ["B4"], ["kcol1"])
-        tt("nrest", T.nm[:, 16:18], T.name[:], T.nm[:, 24:26], ALU.subtract, ["name0", "name1", "nmhi", "nm"], ["nmlo"])
-        quant("qnm", "nm", 0, "nm", 0, 130, ["nm", "nm2", "nm_l", "nm_h", "nmlo", "nmhi"], ["nmq"])
-        for b in range(2):
-            op("A", "rank%d" % b, lambda e, b=b: e.activation(T["junk%d" % b][:], ps(7, 0, 256), AF.Sign, bias=T.kcol[:, b:b + 1], scale=-1.0,
-                                                              accum_out=T[rk][:, b:b + 1]), r=["B7", "kcol%d" % b], w=["junk%d" % b, "%s.%d" % (rk, b)])
-        for b in range(2):
-            ts("onehot%d" % b, T.oh[:, b:512:4], T.place[:], T[rk][:, b:b + 1], None, ALU.is_equal, None, [rk + ".%d" % b] + PL, ["oh%d" % b])
-        quant("qoh", "oh", 0, "oh", 0, 128, ["oh0", "oh1"], ["ohq"])
-        mm("lists", 5, "oh", 0, "nm", 0, 128, ["ohq", "nmq"])
-        ts("offt", T[off][:, 0:1], ps(5, 4, 5), ps(5, 6, 7), None, ALU.add, None, ["B5"], [off + "t"])
-        op("V", "tokq", lambda e: e.tensor_copy(w32(T[win + "q"][:, 0:16]), w32(T.xq[:, 0:256]).indirect(T[off][:, 0:1])), r=["x", off + "t"], w=[win + ".tq"])
-        op("A", "toks", lambda e: e.activation(T[win + "s"][:, 0:16], T.xs[:, 0:256].indirect(T[off][:, 0:1]), AF.Copy), r=["x", off + "t"], w=[win + ".ts"])
-        send("snd_tq", [win + ".tq"], u8(T[win + "q"][:, 0:8]), lambda q: u8(T[win + "q"][:, 16 * slot(r, q):16 * slot(r, q) + 8]), "rt%d" % t)
-        send("snd_ts", [win + ".ts"], T[win + "s"][:, 0:8], lambda q: T[win + "s"][:, 16 * slot(r, q):16 * slot(r, q) + 8], "rt%d" % t)
-        op("X", "arr_t", None, w=["land" + win], ext=(T.sem["rt%d" % t], 2 * lanes * (N - 1)))
-        ts("offc", T[off][:, 2:3], ps(5, 0, 1), ps(5, 2, 3), None, ALU.add, None, ["B5"], [off + "c"])
-        op("V", "candq", lambda e: e.tensor_copy(w32(T[win + "q"][:, 128:144]), w32(T.callq[:, 0:256]).indirect(T[off][:, 2:3])), r=CALL + [off + "c"], w=[win + ".cq"])
-        op("A", "cands", lambda e: e.activation(T[win + "s"][:, 128:144], T.calls[:, 0:256].indirect(T[off][:, 2:3]), AF.Copy), r=CALL + [off + "c"], w=[win + ".cs"])
-        if t + 1 < R:
-            ts("won", T.won[:], T[rk][:], 224.0, -4352.0, ALU.is_gt, ALU.mult, [rk + ".0", rk + ".1"], ["won"])
-            ts("won", T.won[:], T.won[:], 256.0, None, ALU.add, None, ["won"], ["won"])
-            tt("cap", T.cap[:], T.cap[:], T.won[:], ALU.min, ["won", "cap"], ["cap"])
-        else:
-            for s in range(R):
-                for b in range(2):
-                    rs = "rk%d" % s
-                    ts("ohn", T.ohn[:, 64 * s + b:64 * s + 64:4], T.placen[:], T[rs][:, b:b + 1], None, ALU.is_equal, None,
-                       ["ohn", "placen", rs + ".%d" % b], ["ohn%d%d" % (s, b)])
-            quant("qohn", "ohn", 0, "ohn", 0, 128, ["ohn"] + ["ohn%d%d" % (s, b) for s in range(R) for b in range(2)], ["ohnq"])
-            mm("sel0", 6, "nm", 0, "ohn", 0, 128, ["nmq", "ohnq"], True, False)
-            mm("sel1", 6, "nm", 2, "ohn", 0, 128, ["nmq", "ohnq"], False, True)
-            acopy("selrow", T.selrow[0:1, :], T.ps6[0:1, 0:48], ["B6"], ["selrow"])
-            load("S", "st_sel", T.sel[0:1, :], T.selrow[0:1, :], r=["selrow"], w=["out.sel"])
-        if t == 0:
-            for c in range(5):
-                for b in range(2):
-                    acopy("vblk", T.vblk[:, 32 * c + 16 * b:32 * c + 16 * b + 16], T.vrow[:, 16 * c:16 * c + 16],
-                          ["vrow"] + ["vrow.%d" % k for k in range(M)], ["vblk%d%d" % (c, b)])
-            for b in range(4):
-                acopy("eb", T.eb[:, 512 * b + b:512 * b + 512:4], T.ident[:], ["ident"], [EB[b]], scale=0.5)
-            acopy("sq", T.sq[:], ps(0, 128, 256), ["B0"], ["sq"])
-            quant("qzv", "vin", 0, "zt", 0, 128, ["zt"], ["vin.q", "vin.s"])
-            memset("ms_low", T.low[:], -1e29, ["low"])
-            memset("ms_fac", T.fac[:], 0.5, ["fac0", "fac1"])
-            ts("offo", T.offo[:], T.pl[:], 5.0, 4.0, ALU.mult, ALU.add, ["pl"], ["offo"])
-            memset("ms_fac0", T.fac[:, 0:80:5], 0.0, ["fac0"])
-            memset("ms_fac1", T.fac[:, 1:80:5], 1.0, ["fac1"])
-            op("V", "vtr", lambda e: e.transpose(T.vtr[:], T.vblk[:]), r=["vblk%d%d" % (c, b) for c in range(5) for b in range(2)], w=["vtr"])
-            vcopy("offv", T.offv[:, 0:5], T.vtr[:, 0:160:32], ["vtr"], ["offv"])
-            quant("qeb", "eb", 0, "eb", 0, 512, EB, ["ebq"])
         if t == 1:
-            quant("qw", "w", 0, "wt", 0, 256, ["wt"], ["w"])
+            load("S", "ldw", T.wt[:, 512:1024], T.w[:, 512:1024], r=[land], w=["wt1"])
+        for b in range(2):
+            scan("key", T["ks%d" % b][:, 64 - N - 31:64], T.ones[:, 0:N + 31], T[land][:, 2 + b:80:2], T.kinit[:, b:b + 1], ALU.mult, ALU.add,
+                 [land, cnt, "ones", "kinit"], ["ks%d" % b])
+        for b in range(2):
+            flip("row", T.krow[:, 32 * b:32 * b + 32], T["ks%d" % b][:, 32:64], ["ks%d" % b], ["row%d" % b])
+        for q in range(4):
+            (vcopy if q < 2 else acopy)("next", T.krow[32 * q:32 * q + 32, 64:128], T.krow[32 * (q ^ 1):32 * (q ^ 1) + 32, 0:64], ["row0", "row1"], ["next%d" % q])
+        for h in range(2):
+            vcopy("far", T.krow[64 * h:64 * h + 64, 128:256], T.krow[64 - 64 * h:128 - 64 * h, 0:128],
+                  ["row0", "row1", "next%d" % (2 - 2 * h), "next%d" % (3 - 2 * h)], ["far%d" % h])
+        for h in range(2):
+            for b in range(2):
+                rank(b, h)
+        rests(T.placet, PT)
+        hits(T.name, ["name0", "name1"])
+        sums()
+        for h in range(2):
+            total("offt", T[off][64 * h:64 * h + 64, 0:1], [off + "t%d" % h])
+        OT = [off + "t0", off + "t1"]
+        op("V", "tokq", lambda e: e.tensor_copy(w32(T[win + "q"][:, 0:16]), w32(T.xq[:, 0:256]).indirect(T[off][:, 0:1])), r=["x"] + OT, w=[win + ".tq"])
+        op("A", "toks", lambda e: e.activation(T[win + "s"][:, 0:16], T.xs[:, 0:256].indirect(T[off][:, 0:1]), AF.Copy), r=["x"] + OT, w=[win + ".ts"])
+        send("snd_tq", [win + ".tq"], *piece[3 + 2 * t])
+        send("snd_ts", [win + ".ts"], *piece[4 + 2 * t])
+        arrive("landq" + win, "rq%d" % t, N - 1)
+        arrive("lands" + win, "rs%d" % t, N - 1)
+        rests(T.placec, PC)
+        hits(T.num, ["num", "num"])
+        if t + 1 < R:
+            tt("won", T.won[:], T.rk[:, 0:2], T.rk[:, 2:4], ALU.add, ["rk0", "rk1", "rk2", "rk3"], ["won"])
+        sums()
+        if t + 1 < R:
+            ts("won", T.won[:], T.won[:], 255.0 - 2 * M + 1, -4096.0, ALU.is_gt, ALU.mult, ["won"], ["won"])
+        for h in range(2):
+            total("offc", T[off][64 * h:64 * h + 64, 2:3], [off + "c%d" % h])
+        total("selc", T.selc[0:64, t:t + 1], ["selc%d" % t])
+        OC = [off + "c0", off + "c1"]
+        op("V", "candq", lambda e: e.tensor_copy(w32(T[win + "q"][:, 128:144]), w32(T.callq[:, 0:256]).indirect(T[off][:, 2:3])), r=CALL + OC, w=[win + ".cq"])
+        op("A", "cands", lambda e: e.activation(T[win + "s"][:, 128:144], T.calls[:, 0:256].indirect(T[off][:, 2:3]), AF.Copy), r=CALL + OC, w=[win + ".cs"])
+        if t + 1 < R:
+            tt("kinit", T.kinit[:], T.kinit[:], T.won[:], ALU.add, ["won", "kinit"], ["kinit"])
+            memset("ms_land", T["land%d" % (t + 1)][:, OWN:], 0.0, ["cnt%d" % (t + 1)])
+        if t == 1:
+            quant("qw", "w", 0, "wt", 0, 256, ["wt0", "wt1"], ["w"])
         if t:
             pick_out(t - 1)
             products(t - 1)
-        WIN = ["land" + win, win + ".tq", win + ".ts", win + ".cq", win + ".cs", "offv"]
-        op("V", "vinq", lambda e: e.tensor_copy(w32(T.vinq[:, 0:80]), w32(T[win + "q"][:, 0:144]).indirect(T.offv[:, 0:5])), r=WIN, w=["vin.q"])
-        op("A", "vins", lambda e: e.activation(T.vins[:, 0:80], T[win + "s"][:, 0:144].indirect(T.offv[:, 0:5]), AF.Copy), r=WIN, w=["vin.s"])
+            product_copies(t - 1)
+        for a, b in ((0, 2), (2, 5)):
+            op("V", "vinq", lambda e, a=a, b=b: e.tensor_copy(w32(T.vinq[:, 16 * a:16 * b]), w32(T[win + "q"][:, 0:144]).indirect(T.offv[:, a:b])),
+               r=["landq" + win, win + ".tq", win + ".cq", "offv"], w=["vin.q%d" % a])
+        WS = ["lands" + win, win + ".ts", win + ".cs", "offv"]
+        op("A", "vins", lambda e: e.activation(T.vins[:, 0:32], T[win + "s"][:, 0:144].indirect(T.offv[:, 0:2]), AF.Copy), r=WS, w=["vin.s0"])
+        op("V", "vins", lambda e: e.tensor_copy(T.vins[:, 32:80], T[win + "s"][:, 0:144].indirect(T.offv[:, 2:5])), r=WS, w=["vin.s2"])
+        load("S", "st_sel", T.sel[0:1, M * t:M * t + M], T.selc[0:M, t:t + 1], r=["selc%d" % t, "lands" + win], w=["out.sel%d" % t])
+        if t == 0:
+            load("S", "ldw", T.wt[:, 0:512], T.w[:, 0:512], r=["lands" + win], w=["wt0"])
+        if t == R - 1:
+            for o in range(O):
+                load("S", "st_y", T.y[:, ALL * o:ALL * o + M * t], T.yt[:, ALL * o:ALL * o + M * t], r=["yt%d%d" % (s, o) for s in range(t)], w=["out.ya%d" % o])
+            load("S", "st_oc", T.oc[:, 0:4 * M * t], u8(T.voq[:, 0:M * t]), r=["vo.q%d" % s for s in range(t)], w=["out.oca"])
         for b in range(4):
-            mm("dec%d" % b, 4 + b, "eb", 128 * b, "vin", 0, 128, ["ebq", "vin.q", "vin.s"])
+            mm("dec%d" % b, 4 + b, "eb", 128 * b, "vin", 0, 128, [EB[b]] + VIN)
         for b in range(4):
-            op("V", "rec%d" % b, lambda e, b=b: e.tensor_tensor_scan(T.h[:, b:4 * NV:4], T.fac[:], ps(4 + b, 0, NV), 0.0, ALU.mult, ALU.add),
-               r=["B%d" % (4 + b), "fac0", "fac1"], w=["h%d" % b])
+            scan("rec%d" % b, T.h[:, b:4 * NV:4], T.fac[:], ps(4 + b, 0, NV), 0.0, ALU.mult, ALU.add, ["B%d" % (4 + b), "fac0", "fac1"], ["h%d" % b])
         v = "v%d" % t
         quant("qv", v, 0, "h", 0, 128, HT + ["hu", "hc0", "hc1"], [v])
         zmul(v)
@@ -484,18 +572,19 @@ def rank_program(g, core, T, topo):
     for t in range(R):
         one_round(t)
 
-    n = R * M
+    products(R - 1)
     pick_out(R - 1)
     marks(R, 0)
     marks(R, 1)
     turn(R)
-    load("S", "st_oc", T.oc[:, :], u8(T.voq[:, 0:n]), r=["vo.q%d" % t for t in range(R)], w=["out.oc"])
+    load("S", "st_oc", T.oc[:, 4 * (ALL - M):4 * ALL], u8(T.voq[:, ALL - M:ALL]), r=["vo.q%d" % (R - 1)], w=["out.oc"])
     for k in range(4):
-        load("A" if k % 2 else "S", "st_osc%d" % k, T.osc[4 * k:4 * k + 4, :], T.vos[32 * k:32 * k + 4, 0:n], r=["vo.s%d" % t for t in range(R)], w=["out.osc%d" % k])
-    products(R - 1)
-    load("S", "st_y", T.y[:, :], T.yt[:], r=["yt%d%d" % (t, o) for t in range(R) for o in range(O)], w=["out.y"])
-    for a in range(4):
-        load("A" if a % 2 else "S", "st_mk%d" % a, T.mk[0:1, 64 * a:64 * a + 64], T["mt%d" % (R % 2)][32 * a:32 * a + 1, :], r=["mt%d" % (R % 2)], w=["out.mk%d" % a])
-    op("S", "end", None, r=["out.sel", "out.oc", "out.y"] + ["out.osc%d" % k for k in range(4)] + ["out.mk%d" % a for a in range(4)])
+        load("A" if k == 3 else "S", "st_osc%d" % k, T.osc[4 * k:4 * k + 4, :], T.vos[32 * k:32 * k + 4, 0:ALL], r=["vo.s%d" % t for t in range(R)], w=["out.osc%d" % k])
+    product_copies(R - 1)
+    for o in range(O):
+        load("A" if o else "S", "st_y", T.y[:, ALL * o + ALL - M:ALL * o + ALL], T.yt[:, ALL * o + ALL - M:ALL * o + ALL], r=["yt%d%d" % (R - 1, o)], w=["out.y%d" % o])
+    load("S", "st_mk", T.mk[0:1, :], T["mt%d" % (R % 2)][0:128:32, :], r=["mt%d" % (R % 2)], w=["out.mk"])
+    op("S", "end", None, r=["out.sel%d" % t for t in range(R)] + ["out.oca", "out.oc", "out.ya0", "out.ya1", "out.y0", "out.y1", "out.mk"]
+       + ["out.osc%d" % k for k in range(4)])
     _emit(P, g, T)
     g.wait_ge(T.sem.ls, sent[0])

@@ -3,7 +3,9 @@ from concourse.mybir import dt, AluOpType as ALU, ActivationFunctionType as AF
 
 M, R, O = 16, 3, 2
 HELPERS = 2
-RELAY = {"cq": (), "ca": (), "cb": (), "tq": (), "ts": ()}
+FUSE = False
+TOK, CAND = 24, 96
+RELAY = {"ca": (2,)}
 BFT, F32, I32, U16, COD, PLN = "bfloat16", "float32", "int32", "uint16", "float8_e4m3fn_x4", "uint8"
 SCRATCH = {}
 
@@ -17,31 +19,39 @@ def _codes(name, n):
     _sb(name + "s", n, PLN)
 
 
-for _n, _w in (("ctile", 512), ("zt", 516), ("xt", 1024), ("xu", 1024), ("wt", 1024), ("h", 512), ("ind", 512),
-               ("ones", 128), ("ident", 128), ("sg", 128), ("junk0", 256), ("junk1", 256), ("junk2", 512), ("junk3", 64)):
+for _n, _w in (("ctile", 512), ("zt", 516), ("xt", 1024), ("wt", 1024), ("h", 512), ("ind", 512),
+               ("ones", 128), ("ident", 128), ("sg", 128), ("csum", 256), ("over", 512), ("junk0", 256), ("junk1", 256), ("junk2", 512), ("junk3", 128)):
     _sb(_n, _w, BFT)
 for _n, _w in (("mrow", 256), ("d0", 256), ("d1", 256), ("run0", 256), ("run1", 256), ("fac", 80), ("low", 16), ("sq", 128),
                ("bc", 64), ("mtb", 64), ("v16", 16), ("vrow", 80), ("vblk", 160), ("vtr", 160), ("yt", 96), ("name", 2),
-               ("ks0", 64), ("ks1", 64), ("krow", 256), ("kinit", 2), ("num", 2), ("rk", 4), ("won", 2), ("selc", R),
-               ("placet", 32), ("placec", 32), ("rest", 64), ("hit", 64), ("hitt", 64), ("pair", 64), ("part", 1)):
+               ("ks", 80), ("krow", 256), ("kinit", 2), ("num", 2), ("rk", 4), ("won", 2), ("selc", R),
+               ("place", 64), ("rest", 128), ("hit", 128), ("hitt", 128), ("pair", 128), ("part", 2)):
     _sb(_n, _w, F32)
 for _t in range(2):
-    _sb("mk%d" % _t, 96, F32)
-    _sb("mt%d" % _t, 64, F32)
-for _n, _w in (("pn", 2), ("pl", 2), ("vi", 80), ("vi2", 80)):
+    _sb("mk%d" % _t, 32, F32)
+for _n, _w in (("pn", 2), ("pl", 2), ("vi", 80), ("vi2", 80), ("xi", 16)):
     _sb(_n, _w, I32)
+_sb("pl2", 1, F32)
+_sb("offx", 16, U16)
+_sb("offu", 8, U16)
 _sb("offv", 6, U16)
 _sb("offo", 2, U16)
+_sb("offi", 2, U16)
 for _t in range(R):
     _sb("off%d" % _t, 4, U16)
     _sb("land%d" % _t, 80, BFT)
-    _codes("win%d" % _t, 144)
+    _codes("win%d" % _t, 128)
     _codes("v%d" % _t, 128)
-for _n, _w in (("c", 128), ("call", 256), ("x", 256), ("xu", 256), ("w", 256), ("vu", 128), ("vo", 48), ("ind", 128), ("eb", 512), ("vin", 128)):
+for _n, _w in (("c", 128), ("call", 256), ("x", 256), ("xu", 256), ("w", 256), ("vu", 128), ("ub", 128), ("vo", 48), ("ind", 128), ("eb", 512)):
     _codes(_n, _w)
 for _b in range(8):
     SCRATCH["ps%d" % _b] = ("psum", [128, 512], F32)
 SEMAPHORES = ["rc", "ra", "rb"] + ["r%s%d" % (k, t) for k in "nqs" for t in range(R)] + ["ls"] + ["e%d" % i for i in range(130)]
+
+
+TOGETHER = {"above": "ind", "neg": "ind", "key": "key", "row": "row", "half1": "row", "next": "next", "hit0": "hit0", "hit1": "hit1",
+            "part0": "sum0", "pair0": "sum0", "part1": "sum1", "pair1": "sum1", "offt": "offt", "offc": "offc", "vinq": "vinq", "vins": "vins",
+            "rec": "rec", "spa0": "spa0", "spa1": "spa1", "spa2": "spa2", "spa3": "spa3", "bc": "bc", "ub": "ub", "sum": "sum", "xu0": "xu0", "xu1": "xu1", "turnw": "turnw", "vblk": "vblk", "qeb": "qeb"}
 
 
 def _add(P, q, name, fn, r=(), w=(), inc=1, ext=None):
@@ -67,29 +77,42 @@ def _add(P, q, name, fn, r=(), w=(), inc=1, ext=None):
         tags[t]["w"] = i
         tags[t]["r"] = []
     deps.discard(i)
-    ops.append({"q": q, "name": name, "fn": fn, "deps": deps, "inc": inc, "ext": ext})
+    ops.append({"q": q, "name": name, "fn": fn, "deps": deps, "inc": inc, "ext": ext, "set": P["set"] if ext is None and inc == 1 else None})
 
 
 def _emit(P, g, T):
     queues = {"G": g, "V": g.vector, "A": g.scalar, "P": g.tensor, "S": g.sync}
     ops = P["ops"]
     known = {q: 0 for q in queues}
-    done, waits, used = [], [], set()
+    sets = {}
+    for i, o in enumerate(ops):
+        if o["set"] is not None:
+            sets.setdefault(o["set"], []).append(i)
+    done, whole, waits, used = [], [], [], set()
     for i, o in enumerate(ops):
         if o["ext"] is not None:
             done.append(1 << i)
+            whole.append(1 << i)
             waits.append([])
             continue
         need = []
-        for j in sorted(o["deps"], reverse=True):
-            if not known[o["q"]] >> j & 1:
+        open_ = [j for j in o["deps"] if not known[o["q"]] >> j & 1]
+        for j in sorted({sets[ops[j]["set"]][-1] if ops[j]["set"] is not None else j for j in open_}, reverse=True):
+            assert j < i, (o["name"], ops[j]["name"])
+            if whole[j] & ~known[o["q"]]:
                 need.append(j)
-                known[o["q"]] |= done[j]
-        keep = [j for j in need if not any(done[m] >> j & 1 for m in need if m != j)]
-        waits.append(sorted(keep))
+                known[o["q"]] |= whole[j]
+        keep = [j for j in need if any(whole[j] >> d & 1 and not any(whole[m] >> d & 1 for m in need if m != j) for d in open_)]
+        left = [d for d in open_ if not any(whole[m] >> d & 1 for m in keep)]
+        keep += [j for j in need if j not in keep and any(whole[j] >> d & 1 for d in left)]
+        waits.append(sorted(keep, key=lambda j: (ops[j]["ext"] is not None, j)))
         used.update(keep)
         done.append(known[o["q"]] | 1 << i)
-    pool, val = [], {}
+        w = 0
+        for j in (sets[o["set"]] if o["set"] is not None else [i]):
+            w |= done[j] if j <= i else 0
+        whole.append(w)
+    pool, val, taken = [], {}, {}
     for i, o in enumerate(ops):
         if o["ext"] is not None:
             val[i] = o["ext"]
@@ -100,16 +123,20 @@ def _emit(P, g, T):
         if o["fn"] is None:
             continue
         ins = o["fn"](q)
-        if i in used:
+        mates = sets[o["set"]] if o["set"] is not None else [i]
+        if mates[-1] in used:
             dma = o["inc"] > 1
-            free = [s for s in pool if not dma and not s["dma"] and done[i] >> s["last"] & 1]
-            free.sort(key=lambda s: -s["last"])
-            if free:
-                s = free[0]
-            else:
-                s = {"sem": T.sem["e%d" % len(pool)], "n": 0, "dma": dma}
-                pool.append(s)
-            s["last"] = i
+            if i == mates[0]:
+                free = [s for s in pool if not dma and not s["dma"] and all(done[j] & s["last"] == s["last"] for j in mates)]
+                free.sort(key=lambda s: -s["last"])
+                if free:
+                    s = free[0]
+                else:
+                    s = {"sem": T.sem["e%d" % len(pool)], "n": 0, "dma": dma}
+                    pool.append(s)
+                s["last"] = sum(1 << j for j in mates)
+                taken[mates[0]] = s
+            s = taken[mates[0]]
             s["n"] += o["inc"]
             ins.then_inc(s["sem"], o["inc"])
             val[i] = (s["sem"], s["n"])
@@ -134,14 +161,16 @@ def _ways(cores, r, topo):
             del ways[way][:1]
     others += ways["mate"]
     me = cores[r]
-    helpers = [c for c in topo.cores_of(me) if c not in cores and topo.die(c) == topo.die(me)
-               and all(topo.may_write(c, cores[q]) for q in plane)][:HELPERS]
+    helpers = [c for c in topo.cores_of(me) if c not in cores and topo.die(c) == topo.die(me)]
+    reach = {c: [q for q in others if topo.may_write(c, cores[q])] for c in helpers}
+    helpers = sorted(helpers, key=lambda c: len(reach[c]))
+    helpers = [helpers[0], helpers[-1]][:HELPERS]
     far = near = -1
     for q in others:
         far &= topo.mask(me, cores[q])
     for c in helpers:
         near &= topo.mask(me, c)
-    return others, plane, helpers, far, near & ~far
+    return others, [reach[c] for c in helpers], helpers, far, near & ~far
 
 
 def _dst(topo, c):
@@ -165,15 +194,14 @@ def _pieces(T, r, others, plane):
            ("cb", T.cs[:, 0:32], lambda q: T.calls[:, 32 * r:32 * r + 32], "rb", half)]
     for t in range(R):
         wq, ws = T["win%dq" % t], T["win%ds" % t]
-        raw.append(("tq", _u8(wq[:, 0:8]), lambda q, w=wq: _u8(w[:, 16 * _slot(r, q, n):16 * _slot(r, q, n) + 8]), "rq%d" % t, others))
-        raw.append(("ts", ws[:, 0:8], lambda q, w=ws: w[:, 16 * _slot(r, q, n):16 * _slot(r, q, n) + 8], "rs%d" % t, others))
-    out = []
+        raw.append(("tq%d" % t, _u8(wq[:, TOK:TOK + 8]), lambda q, w=wq: _u8(w[:, TOK + 8 * _slot(r, q, n):TOK + 8 * _slot(r, q, n) + 8]), "rq%d" % t, others))
+        raw.append(("ts%d" % t, ws[:, TOK:TOK + 8], lambda q, w=ws: w[:, TOK + 8 * _slot(r, q, n):TOK + 8 * _slot(r, q, n) + 8], "rs%d" % t, others))
+    out = {}
     for kind, src, dst, sem, to in raw:
-        free, shares = [q for q in plane if q in to], []
-        for k in RELAY[kind]:
-            shares.append(free[:k])
-            del free[:k]
-        out.append((src, dst, sem, [q for q in to if not any(q in s for s in shares)], shares))
+        shares = []
+        for k, reach in zip(RELAY.get(kind, ()), plane):
+            shares.append([q for q in reach if q in to and not any(q in s for s in shares)][:k])
+        out[kind] = (src, dst, sem, [q for q in to if not any(q in s for s in shares)], shares)
     return out
 
 
@@ -181,7 +209,7 @@ def _helper(g, core, T, topo, cores, r):
     others, plane, helpers, far, near = _ways(cores, r, topo)
     j = helpers.index(core)
     sent = 0
-    for src, dst, sem, direct, shares in _pieces(T, r, others, plane):
+    for src, dst, sem, direct, shares in _pieces(T, r, others, plane).values():
         share = shares[j] if j < len(shares) else []
         if not share:
             continue
@@ -205,14 +233,15 @@ def rank_program(g, core, T, topo):
             if core in _ways(cores, q, topo)[2]:
                 _helper(g, core, T, topo, cores, q)
         return
-    P = {"ops": [], "tags": {}}
+    P = {"ops": [], "tags": {}, "set": None, "turn": -1}
     others, plane, helpers, mask, near = _ways(cores, r, topo)
     lanes = _count(mask)
     sent = [0]
     piece = _pieces(T, r, others, plane)
 
-    def op(*a, **k):
-        _add(P, *a, **k)
+    def op(q, name, *a, **k):
+        P["set"] = (TOGETHER[name], P["turn"]) if name in TOGETHER else None
+        _add(P, q, name, *a, **k)
 
     u8 = _u8
 
@@ -222,16 +251,19 @@ def rank_program(g, core, T, topo):
     def slot(src, dst):
         return _slot(src, dst, N)
 
-    def send(name, reads, src, dst, sem, direct, shares=()):
-        tr = [RemoteDMATransfer(dst_ids=[_dst(topo, cores[q]) for q in direct], dma_engine_mask=mask, remote_sem=T.sem[sem],
-                                srcs=[src], dsts=[dst(q) for q in direct])]
-        sent[0] += lanes
-        via = [c for c, s in zip(helpers, shares) if s]
+    def send(name, reads, src, dst, sem, direct, shares=(), beside=None):
+        tr = []
+        if direct:
+            tr.append(RemoteDMATransfer(dst_ids=[_dst(topo, cores[q]) for q in direct], dma_engine_mask=mask, remote_sem=T.sem[sem],
+                                        srcs=[src], dsts=[dst(q) for q in direct]))
+            sent[0] += lanes
+        via = [c for c, s in zip(helpers, beside[1][4]) if s] if beside else []
         if via:
-            tr.append(RemoteDMATransfer(dst_ids=[_dst(topo, c) for c in via], dma_engine_mask=near, remote_sem=T.sem[sem],
-                                        srcs=[src], dsts=[src for c in via]))
+            tr.append(RemoteDMATransfer(dst_ids=[_dst(topo, c) for c in via], dma_engine_mask=near, remote_sem=T.sem[beside[1][2]],
+                                        srcs=[beside[0]], dsts=[beside[0] for c in via]))
             sent[0] += _count(near)
-        op("G", name, lambda e: e.remote_dma_fused(tr, local_sem=T.sem.ls), r=reads)
+        if tr:
+            op("G", name, lambda e: e.remote_dma_fused(tr, local_sem=T.sem.ls), r=reads)
 
     def arrive(tag, sem, senders):
         op("X", "arr", None, w=[tag], ext=(T.sem[sem], lanes * senders))
@@ -273,6 +305,9 @@ def rank_program(g, core, T, topo):
     def ramp(name, out, n, first, step, r, w):
         op("A", name, lambda e: e.activation(out, T.v16[:, 0:n], AF.Identity, bias=float(first), scale=float(step)), r=["v16"] + r, w=w)
 
+    def fill(name, out, n, v, w):
+        op("A", name, lambda e: e.activation(out, T.ones[:, 0:n], AF.Identity, bias=float(v), scale=0.0), r=["ones"], w=w)
+
     def load(q, name, out, in_, r=(), w=()):
         op(q, name, lambda e: e.dma_start(out, in_), r=r, w=w, inc=16)
 
@@ -283,7 +318,7 @@ def rank_program(g, core, T, topo):
     order = [None] * M
     for k in range(M):
         i, h = (r - k) % N, k // N
-        order[(i % 4) + 4 * h + 8 * (i // 4)] = k
+        order[(i % 4) + 4 * h + 8 * (1 - i // 4)] = k
     HT = ["h0", "h1", "h2", "h3"]
     EB = ["eb0", "eb1", "eb2", "eb3"]
     VIN = ["vin.q0", "vin.q2", "vin.s0", "vin.s2"]
@@ -292,81 +327,112 @@ def rank_program(g, core, T, topo):
     OWN = 2 * N
     HB = 2 * r // N
     ALL = R * M
+    NAMING = ((0, 0, 0), (0, 1, 0), (1, 0, 0), (0, 0, 128), (1, 1, 0), (0, 1, 128), (1, 0, 128), (1, 1, 128))
 
     load("S", "ldc", T.ctile[:, 0:128], T.c[:, :], w=["ctile"])
-    load("S", "ldx", T.xt[:, :], T.x[:, :], w=["xt"])
-    memset("ms_c", T.ctile[:, 128:512], 0.0, ["ctile0"])
+    load("S", "ldu", T.h[:, 4 * NV:4 * NV + 16], T.u[:, :], w=["hu"])
+    for j in range(2):
+        load("S", "ldx", T.xt[:, 512 * j:512 * j + 512], T.x[:, 512 * j:512 * j + 512], w=["xt%d" % j])
     memset("ms_ones", T.ones[:], 1.0, ["ones"])
-    memset("ms_h", T.h[:], 0.0, HT + ["hu", "hc0", "hc1"])
-    load("S", "ldu", T.h[:, 4 * NV:4 * NV + 4], T.u[:, 0:4], w=["hu"])
+    memset("ms_c", T.ctile[:, 128:512], 0.0, ["ctile0"])
     op("G", "pn", lambda e: e.iota(T.pn[:], [[128, 2]], 0, 1), w=["pn"])
+    op("G", "xi", lambda e: e.iota(T.xi[:], [[1, 2], [32, 8]], 0, 0), w=["xi"])
     op("G", "v16", lambda e: e.iota(T.v16[:], [[1, 16]], 0, 0, allow_small_or_imprecise_dtypes=True), w=["v16"])
-    op("G", "vi", lambda e: e.iota(T.vi[:], [[4, 2], [16, 8], [17, 5]], 256 - 17 - 16 * r, 0), w=["vi"])
+    memset("ms_h", T.h[:, 4 * NV + 16:512], 0.0, ["hc0", "hc1"])
+    ts("pl", T.pl[:], T.pn[:], 15, None, ALU.bitwise_and, None, ["pn"], ["pl"])
+    memset("ms_h", T.h[:, 0:4 * NV], 0.0, HT)
+    for j in range(2):
+        ts("offi", T.offi[:, j:j + 1], T.pl[:, 0:1], 16.0 * j, None, ALU.add, None, ["pl"], ["offi%d" % j])
+    memset("ms_h1", T.h[:, 4 * CV:4 * CV + 2], 1.0, ["hc0"])
+    memset("ms_h2", T.h[:, 4 * CV + 6:4 * CV + 8], 1.0, ["hc1"])
+    memset("offu", T.offu[:], NV, ["offu"])
+    ts("pl2", T.pl2[:], T.pl[:, 0:1], 2.0, None, ALU.mult, None, ["pl"], ["pl2"])
 
     quant("qc", "c", 0, "ctile", 0, 128, ["ctile", "ctile0"], ["c"])
-    for j in range(3):
-        send("snd_c", ["c"], *piece[j])
-    load("S", "ownq", u8(T.callq[:, 32 * r:32 * r + 32]), u8(T.cq[:, 0:32]), r=["c"], w=["own.q"])
-    load("S", "owns", T.calls[:, 32 * r:32 * r + 32], T.cs[:, 0:32], r=["c"], w=["own.s"])
+    send("snd_c", ["c"], *piece["cq"])
+    LATE = bool(RELAY.get("ca"))
+    early, late = ("cb", "ca") if LATE else ("ca", "cb")
+    send("snd_c", ["c"], *piece[early], beside=(piece[late][0], piece[late]))
+    send("snd_c", ["c"], *piece[late])
     arrive("call.q", "rc", N - 1)
     arrive("call.a", "ra", N // 2)
     arrive("call.b", "rb", N // 2 - 1)
     CALL = ["call.q", "call.a", "call.b", "own.q", "own.s"]
 
-    PT, PC = [], ["placec0", "placec1"]
-    for a, b in runs(order):
-        PT.append("placet%d" % a)
-        ramp("place", T.placet[:, a:b], b - a, 255 - 2 * order[a], 2, [], PT[-1:])
-    for j in range(2):
-        ramp("place", T.placec[:, M * j:M * j + M], M, 255, -2, [], [PC[j]])
-    acopy("place", T.placet[:, M:2 * M], T.placet[:, 0:M], list(PT), ["placet."])
-    PT.append("placet.")
+    op("G", "vi", lambda e: e.iota(T.vi[:], [[4, 2], [8, 8], [9, 5]], 128 - 9 - 8 * r, 0), w=["vi"])
     op("G", "ident", lambda e: e.affine_select(T.ident[:], T.ones[:], [[-1, 128]], ALU.is_equal, 0.0, 0, 1), r=["ones"], w=["ident"])
-    memset("ms_h1", T.h[:, 4 * CV:4 * CV + 2], 1.0, ["hc0"])
-    memset("ms_h2", T.h[:, 4 * CV + 6:4 * CV + 8], 1.0, ["hc1"])
-    memset("ms_zt", T.zt[:], 0.0, ["zt"])
-    memset("ms_mk0", T.mk0[:, 32:96], 0.0, ["mk0.0", "mk0.1"])
-    memset("ms_mk1", T.mk1[:, 32:96], 0.0, ["mk1.0", "mk1.1"])
-    quant("qzv", "vin", 0, "zt", 0, 128, ["zt"], VIN)
-    acopy("eb", T.zt[:, 3:515:4], T.ident[:], ["ident"], ["zt"], scale=0.5)
-    ts("vi2", T.vi2[:], T.vi[:], 127, None, ALU.bitwise_and, None, ["vi"], ["vi2"])
-    ts("pl", T.pl[:], T.pn[:], 15, None, ALU.bitwise_and, None, ["pn"], ["pl"])
-    vcopy("vrow", T.vrow[:], T.vi2[:], ["vi2"], ["vrow"])
+    fill("fac", T.fac[:], NV, 0.5, ["fac0", "fac1"])
+    fill("low", T.low[:], M, -1e29, ["low"])
+    for j in range(2):
+        fill("fac", T.fac[:, j:NV:5], M, float(j), ["fac%d" % j])
+    fill("land", T.land0[:, OWN:], 64, 0.0, ["cnt0"])
+    quant("qv", "vu", 0, "h", 0, 128, HT + ["hu", "hc0", "hc1"], VIN)
+    op("V", "ownq", lambda e: e.tensor_copy(w32(T.callq[:, 32 * r:32 * r + 32]), w32(T.cq[:, 0:32]).indirect(T.offi[:, 0:2])), r=["c", "offi0", "offi1"], w=["own.q"])
+    op("A", "owns", lambda e: e.activation(T.calls[:, 32 * r:32 * r + 32], T.cs[:, 0:32].indirect(T.offi[:, 0:2]), AF.Copy), r=["c", "offi0", "offi1"], w=["own.s"])
+    op("V", "ub", lambda e: e.tensor_copy(w32(T.ubq[:, 0:128]), w32(T.vuq[:, 0:128]).indirect(T.offu[:, 0:8])), r=VIN + ["offu"], w=["ub.q"])
+    op("A", "ub", lambda e: e.activation(T.ubs[:, 0:128], T.vus[:, 0:128].indirect(T.offu[:, 0:8]), AF.Copy), r=VIN + ["offu"], w=["ub.s"])
+    for j in range(2):
+        quant("qx", "x", 128 * j, "xt", 512 * j, 128, ["xt%d" % j], ["x%d" % j])
+    X = ["x0", "x1"]
+    mm("m0", 6, "ub", 0, "x", 0, 256, X + ["ub.q", "ub.s"])
+    ts("offx", T.offx[:], T.xi[:], T.pl2[:], None, ALU.add, None, ["xi", "pl2"], ["offx"])
+    acopy("m0", T.mrow[:], ps(6, 0, 256), ["B6"], ["mrow%d.%d" % (a, q) for a in range(4) for q in range(4)])
+    for b in range(2):
+        op("V", "xu%d" % b, lambda e, b=b: e.tensor_copy(w32(T.xuq[:, 128 * b:128 * b + 128]), w32(T.xq[:, 0:256]).indirect(T.offx[:, 8 * b:8 * b + 8])),
+           r=X + ["offx"], w=["xu.q%d" % b])
+        op("A", "xu%d" % b, lambda e, b=b: e.activation(T.xus[:, 128 * b:128 * b + 128], T.xs[:, 0:256].indirect(T.offx[:, 8 * b:8 * b + 8]), AF.Copy),
+           r=X + ["offx"], w=["xu.s%d" % b])
     vcopy("num", T.num[:], T.pn[:], ["pn"], ["num"])
-    memset("ms_land", T.land0[:, OWN:], 0.0, ["cnt0"])
-    ramp("vrowk", T.vrow[:, 0:NV:5], M, 128, 1, ["vrow"], ["vrow"])
-    for a in range(4):
-        for b in range(2):
-            (vcopy if b else acopy)("xu", T.xu[:, 512 * b + 128 * a:512 * b + 128 * a + 128], T.xt[:, 256 * a + 128 * b:256 * a + 128 * b + 128],
-                                    ["xt"], ["xu%d%d" % (a, b)])
-    quant("qv", "vu", 0, "h", 0, 128, HT + ["hu", "hc0", "hc1"], ["vu"])
-    quant("qxu", "xu", 0, "xu", 0, 256, ["xu%d%d" % (a, b) for a in range(4) for b in range(2)], ["xuq"])
-    for c in range(5):
-        for b in range(2):
-            acopy("vblk", T.vblk[:, 32 * c + 16 * b:32 * c + 16 * b + 16], T.vrow[:, 16 * c:16 * c + 16], ["vrow"], ["vblk%d%d" % (c, b)])
+    ts("kinit", T.kinit[:], T.pn[:], -1.0 / 256, 255.0 / 256, ALU.mult, ALU.add, ["pn"], ["kinit"])
+    PT, PC = [], ["placec0", "placec1"]
+
+    def places():
+        for a, b in runs(order):
+            PT.append("placet%d" % a)
+            ramp("place", T.place[:, a:b], b - a, 255 - 2 * order[a], 2, [], PT[-1:])
+        for j in range(2):
+            ramp("place", T.place[:, M * j + 32:M * j + 32 + M], M, 255, -2, [], [PC[j]])
+        acopy("place", T.place[:, M:2 * M], T.place[:, 0:M], list(PT), ["placet."])
+        PT.append("placet.")
+
+    def remaking_list():
+        ramp("vrowk", T.vrow[:, 0:NV:5], M, CAND, 1, ["vrow"], ["vrow"])
+        for c in range(5):
+            for b in range(2):
+                acopy("vblk", T.vblk[:, 32 * c + 16 * b:32 * c + 16 * b + 16], T.vrow[:, 16 * c:16 * c + 16], ["vrow"], ["vblk%d%d" % (c, b)])
+
+    def remaking_offsets():
+        flip("vtr", T.vtr[:], T.vblk[:], ["vblk%d%d" % (c, b) for c in range(5) for b in range(2)], ["vtr"])
+        ts("offo", T.offo[:], T.pl[:], 5.0, 4.0, ALU.mult, ALU.add, ["pl"], ["offo"])
+        vcopy("offv", T.offv[:, 0:5], T.vtr[:, 0:160:32], ["vtr"], ["offv"])
+
+    def one_hot(bb):
+        for b in bb:
+            quant("qeb", "eb", 128 * b, "zt", 3 - b, 128, ["zt"], [EB[b]])
 
     def zmul(v):
         for b in range(2):
-            mm("z%d" % b, 4 + b, "xu", 128 * b, v, 0, 128, ["xuq", v])
+            mm("z%d" % b, 4 + b, "xu", 128 * b, v, 0, 128, ["xu.q%d" % b, "xu.s%d" % b] + (VIN if v == "vu" else [v]))
 
     def mk(t, b):
-        return T["mk%d" % (t % 2)][:, 32 * b + 32:32 * b + 33]
+        return T["mk%d" % (t % 2)][:, 30 + b:31 + b]
 
     def marks(t, b):
         q = "mk%d.%d" % (t % 2, b)
         if t == 0:
             vcopy("mark%d" % b, mk(0, b), ps(4 + b, NV, NV + 1), ["B%d" % (4 + b)], [q])
         else:
-            scan("mark%d" % b, T["mk%d" % (t % 2)][:, 32 * b + 33 - M:32 * b + 33], T["ps%d" % (4 + b)][:, 4:NV:5], T.low[:], mk(t - 1, b),
+            scan("mark%d" % b, T["mk%d" % (t % 2)][:, b:2 * M:2], T["ps%d" % (4 + b)][:, 4:NV:5], T.low[:], mk(t - 1, b),
                  ALU.max, ALU.max, ["B%d" % (4 + b), "low", "mk%d.%d" % ((t - 1) % 2, b)], [q])
 
     def turn(t):
-        flip("turn", T["mt%d" % (t % 2)][:], T["mk%d" % (t % 2)][:, 32:96], ["mk%d.0" % (t % 2), "mk%d.1" % (t % 2)], ["mt%d" % (t % 2)])
+        for b in range(2):
+            flip("turnw", T.mtb[:, b:64:2], T.bc[:, 32 * b:32 * b + 32], ["bc%d" % b], ["mtb%d" % b])
 
     def spread(t, aa):
         for a in aa:
-            op("G", "spread%d" % a, lambda e, a=a: e.partition_broadcast(T.mrow[:, 64 * a:64 * a + 64], T["mt%d" % (t % 2)][32 * a:32 * a + 1, :], 128),
-               r=["mt%d" % (t % 2)], w=["mrow%d.%d" % (a, q) for q in range(4)])
+            op("G", "spread%d" % a, lambda e, a=a: e.partition_broadcast(T.mrow[:, 64 * a:64 * a + 64], T.mtb[32 * a:32 * a + 1, :], 128),
+               r=["mtb0", "mtb1"], w=["mrow%d.%d" % (a, q) for q in range(4)])
 
     def widen(t):
         for b in range(2):
@@ -375,33 +441,34 @@ def rank_program(g, core, T, topo):
     def spread_a(aa):
         for a in aa:
             for q in range(4):
-                acopy("spa", T.mrow[32 * q:32 * q + 32, 64 * a:64 * a + 64], T.mtb[32 * a:32 * a + 32, :], ["mtb"], ["mrow%d.%d" % (a, q)])
+                acopy("spa%d" % a, T.mrow[32 * q:32 * q + 32, 64 * a:64 * a + 64], T.mtb[32 * a:32 * a + 32, :], ["mtb0", "mtb1"], ["mrow%d.%d" % (a, q)])
 
     zmul("vu")
-    quant("qx", "x", 0, "xt", 0, 256, ["xt"], ["x"])
+    ts("vi2", T.vi2[:], T.vi[:], 63, None, ALU.bitwise_and, None, ["vi"], ["vi2"])
+    memset("ms_zt", T.zt[:], 0.0, ["zt"])
+    ts("vrow", T.vrow[:], T.vi2[:], float(TOK), None, ALU.add, None, ["vi2"], ["vrow"])
     marks(0, 0)
     marks(0, 1)
-    ts("kinit", T.kinit[:], T.num[:], -1.0 / 256, 255.0 / 256, ALU.mult, ALU.add, ["num"], ["kinit"])
-    turn(0)
-    spread(0, (0, 1, 2, 3))
-    memset("ms_low", T.low[:], -1e29, ["low"])
-    memset("ms_fac", T.fac[:], 0.5, ["fac0", "fac1"])
-    ts("offo", T.offo[:], T.pl[:], 5.0, 4.0, ALU.mult, ALU.add, ["pl"], ["offo"])
-    memset("ms_fac0", T.fac[:, 0:80:5], 0.0, ["fac0"])
-    memset("ms_fac1", T.fac[:, 1:80:5], 1.0, ["fac1"])
-    flip("vtr", T.vtr[:], T.vblk[:], ["vblk%d%d" % (c, b) for c in range(5) for b in range(2)], ["vtr"])
-    quant("qeb", "eb", 0, "zt", 3, 128, ["zt"], [EB[0]])
-    vcopy("offv", T.offv[:, 0:5], T.vtr[:, 0:160:32], ["vtr"], ["offv"])
-    for b in range(1, 4):
-        quant("qeb", "eb", 128 * b, "zt", 3 - b, 128, ["zt"], [EB[b]])
+    places()
+    acopy("eb", T.zt[:, 3:515:4], T.ident[:], ["ident"], ["zt"], scale=0.5)
+    remaking_list()
+    for t in range(R if FUSE else 0):
+        op("V", "padq", lambda e, t=t: e.tensor_copy(w32(T["win%dq" % t][:, 0:16]), w32(T.xq[:, 0:256]).indirect(T.offi[:, 0:1])), r=X + ["offi0"], w=["win%d.pq" % t])
+        op("A", "pads", lambda e, t=t: e.activation(T["win%ds" % t][:, 0:16], T.xs[:, 0:256].indirect(T.offi[:, 0:1]), AF.Copy), r=X + ["offi0"], w=["win%d.ps" % t])
 
-    def above(t, b, k, bank, a):
-        ts("above", T.ind[:, 2 * k + b:512:4], ps(bank, a, a + 128), mk(t, b), None, ALU.is_gt, None,
-           ["B%d" % bank, "mk%d.%d" % (t % 2, b)], ["ind%d%d" % (b, k)])
+    def above(t, b, k):
+        ts("above", T.ind[:, 2 * k + b:512:4], ps(b, 128 * k, 128 * k + 128), mk(t, b), None, ALU.is_gt, None,
+           ["B%d" % b, "mk%d.%d" % (t % 2, b)], ["ind%d%d" % (b, k)])
 
     def above_a(t):
-        op("A", "sgn", lambda e: e.activation(T.sg[:], T.sq[:], AF.Sign, bias=mk(t, 0), scale=-1.0), r=["sq", "mk%d.0" % (t % 2)], w=["sg"])
-        op("A", "neg", lambda e: e.activation(T.ind[:, 2:512:4], T.sg[:], AF.Relu, scale=-1.0), r=["sg"], w=["ind01"])
+        for a in (0, 64):
+            op("A", "sgn", lambda e, a=a: e.activation(T.sg[:, a:a + 64], T.sq[:, a:a + 64], AF.Sign, bias=mk(t, 0), scale=-1.0),
+               r=["sq0", "mk%d.0" % (t % 2)], w=["sg%d" % a])
+
+    def above_b(t):
+        for a in (0, 64):
+            op("A", "neg", lambda e, a=a: e.activation(T.ind[:, 2 - 2 * HB + 4 * a:4 * a + 256:4], T.sg[:, a:a + 64], AF.Relu, scale=-1.0),
+               r=["sg%d" % a], w=["ind0%d%s" % (1 - HB, "." if a else "")])
 
     def pieces(what, b, lo, hi):
         return ["%s%d.%d" % (what, b, h) for h in range(lo // 64, hi // 64)]
@@ -417,6 +484,10 @@ def rank_program(g, core, T, topo):
     def name_at(b):
         op("A", "name%d" % b, lambda e: e.activation(T["junk%d" % b][:], T["run%d" % b][:], AF.Sign, bias=T["run%d" % b][:, 255:256], scale=-1.0,
                                                      accum_out=T.name[:, b:b + 1]), r=pieces("run", b, 0, 256), w=["junk%d" % b, "name%d" % b])
+
+    def count_sums(b1, b2):
+        for b, a, tags in ((b1, 0, ["over0"]), (b2, 256, ["over10", "over11"])):
+            scan("sum", T.csum[:, b:256:2], T.over[:, a:a + 128], T.over[:, a + 128:a + 256], 0.0, ALU.add, ALU.add, tags, ["csum%d" % b])
 
     def pick_out(t):
         v = "v%d" % t
@@ -434,114 +505,133 @@ def rank_program(g, core, T, topo):
 
     def rank(b, h):
         j = 2 * h + b
-        op("A", "rank", lambda e: e.activation(T.junk2[:, 128 * j:128 * j + 128], T.krow[:, 128 * h:128 * h + 128], AF.Sign, bias=T["ks%d" % b][:, 63:64],
+        op("A", "rank", lambda e: e.activation(T.junk2[:, 128 * j:128 * j + 128], T.krow[:, 128 * h:128 * h + 128], AF.Sign, bias=T.ks[:, 40 - b:41 - b],
                                                scale=-1.0, accum_out=T.rk[:, j:j + 1]),
-           r=["ks%d" % b] + (["far0", "far1"] if h else ["row0", "row1"] + ["next%d" % q for q in range(4)]), w=["junk2.%d" % j, "rk%d" % j])
+           r=["ks%d" % b] + (["next%d.%d" % (q, d) for q in range(4) for d in (1, 3)] if h else ["row", "half0", "half1"]), w=["junk2.%d" % j, "rk%d" % j])
 
-    def rests(place, tags):
-        for b in range(2):
-            ts("rest", T.rest[:, 32 * b:32 * b + 32], place[:], T.rk[:, b:b + 1], None, ALU.subtract, None, tags + ["rk%d" % b], ["rest%d" % b])
+    def rest(b, tags):
+        ts("rest", T.rest[:, 64 * b:64 * b + 64], T.place[:], T.rk[:, b:b + 1], None, ALU.subtract, None, tags + ["rk%d" % b], ["rest%d" % b])
 
-    def hits(value, tags):
-        for b in range(2):
-            ts("hit", T.hit[:, 32 * b:32 * b + 32], T.rest[:, 32 * b:32 * b + 32], T.rk[:, 2 + b:3 + b], value[:, b:b + 1], ALU.is_equal, ALU.mult,
-               ["rest%d" % b, "rk%d" % (2 + b), tags[b]], ["hit%d" % b])
-        flip("hitt", T.hitt[:], T.hit[:], ["hit0", "hit1"], ["hitt"])
+    def hit(j, b):
+        a = 64 * j + 32 * b
+        ts("hit%d" % j, T.hit[:, a:a + 32], T.rest[:, 64 * b + 32 * j:64 * b + 32 * j + 32], T.rk[:, 2 + b:3 + b], (T.num if j else T.name)[:, b:b + 1],
+           ALU.is_equal, ALU.mult, ["rest%d" % b, "rk%d" % (2 + b), "num" if j else "name%d" % b], ["hit%d%d" % (j, b)])
 
-    def sums():
-        op("A", "part", lambda e: e.activation(T.junk3[:], T.hitt[:], AF.Copy, accum_out=T.part[:]), r=["hitt"], w=["junk3", "part"])
+    def hit_turn(j):
+        flip("hitt", T.hitt[:, 64 * j:64 * j + 64], T.hit[:, 64 * j:64 * j + 64], ["hit%d0" % j, "hit%d1" % j], ["hitt%d" % j])
+
+    def sums(j):
+        c = slice(64 * j, 64 * j + 64)
+        op("A", "part%d" % j, lambda e: e.activation(T.junk3[:, c], T.hitt[:, c], AF.Copy, accum_out=T.part[:, j:j + 1]), r=["hitt%d" % j], w=["junk3%d" % j, "part%d" % j])
         for q in range(2):
             a = 32 * (1 - q)
-            scan("pair", T.pair[32 * q:32 * q + 32, :], T.hitt[a:a + 32, :], T.hitt[a + 64:a + 96, :], 0.0, ALU.add, ALU.add, ["hitt"], ["pair%d" % q])
+            scan("pair%d" % j, T.pair[32 * q:32 * q + 32, c], T.hitt[a:a + 32, c], T.hitt[a + 64:a + 96, c], 0.0, ALU.add, ALU.add, ["hitt%d" % j], ["pair%d%d" % (j, q)])
 
-    def total(name, out, w):
-        ts(name, out, T.part[0:64, :], T.part[64:128, :], T.pair[0:64, 63:64], ALU.add, ALU.add, ["part", "pair0", "pair1"], w)
+    def total(j, name, out, w):
+        ts(name, out, T.part[0:64, j:j + 1], T.part[64:128, j:j + 1], T.pair[0:64, 64 * j + 63:64 * j + 64], ALU.add, ALU.add,
+           ["part%d" % j, "pair%d0" % j, "pair%d1" % j], w)
 
     def one_round(t):
         win, off, cnt, land = "win%d" % t, "off%d" % t, "cnt%d" % t, "land%d" % t
+        P["turn"] = t
         if t == 0:
-            for b in range(2):
-                mm("sb", 4 + b, "xu", 128 * b, "call", 128 * (1 - HB), 128, ["xuq", "call.q", "call.a"])
-            for b in range(2):
-                above(t, b, 1 - HB, 4 + b, 0)
-            for b in range(2):
-                mm("sb", b, "xu", 128 * b, "call", 128 * HB, 128, ["xuq"] + CALL)
-            for b in range(2):
-                above(t, b, HB, b, 0)
+            b1, b2 = (HB, 1 - HB) if LATE else (1 - HB, HB)
+            need = {HB: ["call.q", "call.b", "own.q", "own.s"], 1 - HB: ["call.q", "call.a"]}
+            MR = ["mrow%d.%d" % (a, q) for a in range(4) for q in range(4)]
+            mm("sa", 2 + b1, "call", 128 * b1, "x", 0, 256, X + need[b1])
+            tt("over", T.over[:, 0:256], ps(2 + b1, 0, 256), T.mrow[:], ALU.is_gt, ["B%d" % (2 + b1)] + MR, ["over0"])
+            for j in range(2):
+                mm("sa", 4 + j, "call", 128 * b2, "x", 128 * j, 128, X + need[b2])
+            mm("sa", 2 + b2, "call", 128 * b2, "x", 0, 256, X + need[b2])
+            for j in range(2):
+                tt("over", T.over[:, 256 + 128 * j:384 + 128 * j], ps(4 + j, 0, 128), T.mrow[:, 128 * j:128 * j + 128], ALU.is_gt, ["B%d" % (4 + j)] + MR, ["over1%d" % j])
+            count_sums(b1, b2)
+            own, tags = T.csum[:, 254:256], ["csum0", "csum1"]
+            acopy("cnt", T[land][:, OWN:OWN + 2], own, tags, [cnt])
         else:
             marks(t, 0)
             above_a(t)
             marks(t, 1)
-            above(t, 0, 0, 0, 0)
-            above(t, 1, 0, 1, 0)
-            above(t, 1, 1, 1, 128)
-            turn(t)
+            above(t, 0, HB)
+            above(t, 1, HB)
+            above(t, 1, 1 - HB)
             widen(t)
-        quant("qind", "ind", 0, "ind", 0, 128, ["ind00", "ind01", "ind10", "ind11"], ["indq"])
-        if t:
+            above_b(t)
+            turn(t)
+            quant("qind", "ind", 0, "ind", 0, 128, ["ind00", "ind01", "ind10", "ind11", "ind0%d." % (1 - HB)], ["indq"])
             spread(t, (0,))
-            flip("turnw", T.mtb[:], T.bc[:], ["bc0", "bc1"], ["mtb"])
             spread_a((1, 2, 3))
-        mm("cnt", 6, "ind", 0, "vu", 0, 128, ["indq", "vu"])
-        vcopy("cnt", T[land][:, OWN:OWN + 2], ps(6, CV, CV + 2), ["B6"], [cnt])
-        send("snd_n", [cnt], T[land][:, OWN:OWN + 2], lambda q: T[land][:, 2 * slot(r, q):2 * slot(r, q) + 2], "rn%d" % t, others)
+            mm("cnt", 6, "ind", 0, "vu", 0, 128, ["indq"] + VIN)
+            vcopy("cnt", T[land][:, OWN:OWN + 2], ps(6, CV, CV + 2), ["B6"], [cnt])
+            own, tags = T[land][:, OWN:OWN + 2], [cnt]
+        send("snd_n", tags, own, lambda q: T[land][:, 2 * slot(r, q):2 * slot(r, q) + 2], "rn%d" % t, others)
         arrive(land, "rn%d" % t, N - 1)
         if t == 0:
             for b in range(2):
-                mm("sa%d" % b, 2 + b, "call", 128 * b, "x", 0, 256, ["x"] + CALL)
-            for b in range(2):
-                mm("sb%d" % b, b, "xu", 128 * b, "call", 0, 256, ["xuq"] + CALL)
-            acopy("sq", T.sq[:], ps(0, 128, 256), ["B0"], ["sq"])
-        for lo, hi in (((0, 128), (128, 256)) if t else ((0, 256),)):
-            for b in range(2):
-                name_diff(b, lo, hi)
-            for b in range(2):
-                name_run(b, lo, hi)
-        name_at(0)
-        name_at(1)
+                mm("sb", b, "xu", 128 * b, "call", 0, 256, ["xu.q%d" % b, "xu.s%d" % b] + CALL)
+            acopy("sq", T.sq[:], ps(0, 128 - 128 * HB, 256 - 128 * HB), ["B0"], ["sq0"])
+            for b in (b1, b2):
+                name_diff(b, 0, 256)
+            for b in (b1, b2):
+                name_run(b, 0, 256)
+        else:
+            for f, b, lo in NAMING:
+                (name_run if f else name_diff)(b, lo, lo + 128)
+        for b in ((0, 1) if t else (b1, b2)):
+            name_at(b)
         if t == 1:
             load("S", "ldw", T.wt[:, 512:1024], T.w[:, 512:1024], r=[land], w=["wt1"])
         for b in range(2):
-            scan("key", T["ks%d" % b][:, 64 - N - 31:64], T.ones[:, 0:N + 31], T[land][:, 2 + b:80:2], T.kinit[:, b:b + 1], ALU.mult, ALU.add,
+            scan("key", T.ks[:, 1:40] if b else T.ks[:, 78:39:-1], T.ones[:, 0:N + 31], T[land][:, 2 + b:80:2], T.kinit[:, b:b + 1], ALU.mult, ALU.add,
                  [land, cnt, "ones", "kinit"], ["ks%d" % b])
-        for b in range(2):
-            flip("row", T.krow[:, 32 * b:32 * b + 32], T["ks%d" % b][:, 32:64], ["ks%d" % b], ["row%d" % b])
-        for q in range(4):
-            (vcopy if q < 2 else acopy)("next", T.krow[32 * q:32 * q + 32, 64:128], T.krow[32 * (q ^ 1):32 * (q ^ 1) + 32, 0:64], ["row0", "row1"], ["next%d" % q])
-        for h in range(2):
-            vcopy("far", T.krow[64 * h:64 * h + 64, 128:256], T.krow[64 - 64 * h:128 - 64 * h, 0:128],
-                  ["row0", "row1", "next%d" % (2 - 2 * h), "next%d" % (3 - 2 * h)], ["far%d" % h])
+        KS = ["ks0", "ks1"]
+        flip("row", T.krow[:, 0:64], T.ks[:, 8:72], KS, ["row"])
+        for h in (1, 0):
+            flip("half%d" % h, T.krow[64 * h:64 * h + 64, 64:128], T.ks[64 - 64 * h:128 - 64 * h, 8:72], KS, ["half%d" % h])
+        acopy("next", T.krow[96:128, 128:256], T.krow[64:96, 0:128], ["row", "half1"], ["next3.1", "next3.3"])
+        for q in range(3):
+            for d in (1, 3):
+                flip("next", T.krow[32 * q:32 * q + 32, 96 + 32 * d:160 + 32 * d], T.ks[32 * (q ^ d):32 * (q ^ d) + 32, 8:72], KS, ["next%d.%d" % (q, d)])
         for h in range(2):
             for b in range(2):
                 rank(b, h)
-        rests(T.placet, PT)
-        hits(T.name, ["name0", "name1"])
-        sums()
+        for b in range(2):
+            rest(b, PT + PC)
+        for j, b in ((0, 0), (1, 0), (0, 1), (1, 1)):
+            hit(j, b)
+        for j in range(2):
+            hit_turn(j)
+        for j in range(2):
+            sums(j)
         for h in range(2):
-            total("offt", T[off][64 * h:64 * h + 64, 0:1], [off + "t%d" % h])
+            total(0, "offt", T[off][64 * h:64 * h + 64, 0:1], [off + "t%d" % h])
+        for h in range(2):
+            total(1, "offc", T[off][64 * h:64 * h + 64, 2:3], [off + "c%d" % h])
         OT = [off + "t0", off + "t1"]
-        op("V", "tokq", lambda e: e.tensor_copy(w32(T[win + "q"][:, 0:16]), w32(T.xq[:, 0:256]).indirect(T[off][:, 0:1])), r=["x"] + OT, w=[win + ".tq"])
-        op("A", "toks", lambda e: e.activation(T[win + "s"][:, 0:16], T.xs[:, 0:256].indirect(T[off][:, 0:1]), AF.Copy), r=["x"] + OT, w=[win + ".ts"])
-        send("snd_tq", [win + ".tq"], *piece[3 + 2 * t])
-        send("snd_ts", [win + ".ts"], *piece[4 + 2 * t])
+        op("V", "tokq", lambda e: e.tensor_copy(w32(T[win + "q"][:, 16:32]), w32(T.xq[:, 0:256]).indirect(T[off][:, 0:1])), r=X + OT, w=[win + ".tq"])
+        op("A", "toks", lambda e: e.activation(T[win + "s"][:, 16:32], T.xs[:, 0:256].indirect(T[off][:, 0:1]), AF.Copy), r=X + OT, w=[win + ".ts"])
+        if FUSE:
+            send("snd_tq", [win + ".tq", win + ".ts", win + ".ps"], *piece["tq%d" % t], beside=(T[win + "s"][:, 0:32], piece["ts%d" % t]))
+            send("snd_ts", [win + ".ts"], *piece["ts%d" % t])
+        else:
+            send("snd_tq", [win + ".tq"], *piece["tq%d" % t])
+            send("snd_ts", [win + ".ts"], *piece["ts%d" % t], beside=(piece["ts%d" % t][0], piece["ts%d" % t]))
         arrive("landq" + win, "rq%d" % t, N - 1)
         arrive("lands" + win, "rs%d" % t, N - 1)
-        rests(T.placec, PC)
-        hits(T.num, ["num", "num"])
         if t + 1 < R:
             tt("won", T.won[:], T.rk[:, 0:2], T.rk[:, 2:4], ALU.add, ["rk0", "rk1", "rk2", "rk3"], ["won"])
-        sums()
+        OC = [off + "c0", off + "c1"]
+        op("V", "candq", lambda e: e.tensor_copy(w32(T[win + "q"][:, CAND:CAND + M]), w32(T.callq[:, 0:256]).indirect(T[off][:, 2:3])), r=CALL + OC, w=[win + ".cq"])
+        total(1, "selc", T.selc[0:64, t:t + 1], ["selc%d" % t])
         if t + 1 < R:
             ts("won", T.won[:], T.won[:], 255.0 - 2 * M + 1, -4096.0, ALU.is_gt, ALU.mult, ["won"], ["won"])
-        for h in range(2):
-            total("offc", T[off][64 * h:64 * h + 64, 2:3], [off + "c%d" % h])
-        total("selc", T.selc[0:64, t:t + 1], ["selc%d" % t])
-        OC = [off + "c0", off + "c1"]
-        op("V", "candq", lambda e: e.tensor_copy(w32(T[win + "q"][:, 128:144]), w32(T.callq[:, 0:256]).indirect(T[off][:, 2:3])), r=CALL + OC, w=[win + ".cq"])
-        op("A", "cands", lambda e: e.activation(T[win + "s"][:, 128:144], T.calls[:, 0:256].indirect(T[off][:, 2:3]), AF.Copy), r=CALL + OC, w=[win + ".cs"])
+        op("A", "cands", lambda e: e.activation(T[win + "s"][:, CAND:CAND + M], T.calls[:, 0:256].indirect(T[off][:, 2:3]), AF.Copy), r=CALL + OC, w=[win + ".cs"])
         if t + 1 < R:
             tt("kinit", T.kinit[:], T.kinit[:], T.won[:], ALU.add, ["won", "kinit"], ["kinit"])
-            memset("ms_land", T["land%d" % (t + 1)][:, OWN:], 0.0, ["cnt%d" % (t + 1)])
+            fill("land", T["land%d" % (t + 1)][:, OWN:], 64, 0.0, ["cnt%d" % (t + 1)])
+        if t == 0:
+            remaking_offsets()
+            one_hot((0, 1, 2, 3))
         if t == 1:
             quant("qw", "w", 0, "wt", 0, 256, ["wt0", "wt1"], ["w"])
         if t:
@@ -549,11 +639,11 @@ def rank_program(g, core, T, topo):
             products(t - 1)
             product_copies(t - 1)
         for a, b in ((0, 2), (2, 5)):
-            op("V", "vinq", lambda e, a=a, b=b: e.tensor_copy(w32(T.vinq[:, 16 * a:16 * b]), w32(T[win + "q"][:, 0:144]).indirect(T.offv[:, a:b])),
-               r=["landq" + win, win + ".tq", win + ".cq", "offv"], w=["vin.q%d" % a])
-        WS = ["lands" + win, win + ".ts", win + ".cs", "offv"]
-        op("A", "vins", lambda e: e.activation(T.vins[:, 0:32], T[win + "s"][:, 0:144].indirect(T.offv[:, 0:2]), AF.Copy), r=WS, w=["vin.s0"])
-        op("V", "vins", lambda e: e.tensor_copy(T.vins[:, 32:80], T[win + "s"][:, 0:144].indirect(T.offv[:, 2:5])), r=WS, w=["vin.s2"])
+            op("V", "vinq", lambda e, a=a, b=b: e.tensor_copy(w32(T.vuq[:, 16 * a:16 * b]), w32(T[win + "q"][:, 0:128]).indirect(T.offv[:, a:b])),
+               r=["landq" + win, win + ".tq", win + ".cq", win + ".pq", "offv"], w=["vin.q%d" % a])
+        WS = ["lands" + win, win + ".ts", win + ".cs", win + ".ps", "offv"]
+        op("A", "vins", lambda e: e.activation(T.vus[:, 0:32], T[win + "s"][:, 0:128].indirect(T.offv[:, 0:2]), AF.Copy), r=WS, w=["vin.s0"])
+        op("V", "vins", lambda e: e.tensor_copy(T.vus[:, 32:80], T[win + "s"][:, 0:128].indirect(T.offv[:, 2:5])), r=WS, w=["vin.s2"])
         load("S", "st_sel", T.sel[0:1, M * t:M * t + M], T.selc[0:M, t:t + 1], r=["selc%d" % t, "lands" + win], w=["out.sel%d" % t])
         if t == 0:
             load("S", "ldw", T.wt[:, 0:512], T.w[:, 0:512], r=["lands" + win], w=["wt0"])
@@ -562,28 +652,28 @@ def rank_program(g, core, T, topo):
                 load("S", "st_y", T.y[:, ALL * o:ALL * o + M * t], T.yt[:, ALL * o:ALL * o + M * t], r=["yt%d%d" % (s, o) for s in range(t)], w=["out.ya%d" % o])
             load("S", "st_oc", T.oc[:, 0:4 * M * t], u8(T.voq[:, 0:M * t]), r=["vo.q%d" % s for s in range(t)], w=["out.oca"])
         for b in range(4):
-            mm("dec%d" % b, 4 + b, "eb", 128 * b, "vin", 0, 128, [EB[b]] + VIN)
+            mm("dec%d" % b, 4 + b, "eb", 128 * b, "vu", 0, 128, [EB[b]] + VIN)
         for b in range(4):
-            scan("rec%d" % b, T.h[:, b:4 * NV:4], T.fac[:], ps(4 + b, 0, NV), 0.0, ALU.mult, ALU.add, ["B%d" % (4 + b), "fac0", "fac1"], ["h%d" % b])
+            scan("rec", T.h[:, b:4 * NV:4], T.fac[:], ps(4 + b, 0, NV), 0.0, ALU.mult, ALU.add, ["B%d" % (4 + b), "fac0", "fac1"], ["h%d" % b])
         v = "v%d" % t
         quant("qv", v, 0, "h", 0, 128, HT + ["hu", "hc0", "hc1"], [v])
+        if t == R - 1:
+            products(t)
         zmul(v)
 
     for t in range(R):
         one_round(t)
 
-    products(R - 1)
     pick_out(R - 1)
     marks(R, 0)
     marks(R, 1)
-    turn(R)
     load("S", "st_oc", T.oc[:, 4 * (ALL - M):4 * ALL], u8(T.voq[:, ALL - M:ALL]), r=["vo.q%d" % (R - 1)], w=["out.oc"])
     for k in range(4):
         load("A" if k == 3 else "S", "st_osc%d" % k, T.osc[4 * k:4 * k + 4, :], T.vos[32 * k:32 * k + 4, 0:ALL], r=["vo.s%d" % t for t in range(R)], w=["out.osc%d" % k])
     product_copies(R - 1)
     for o in range(O):
         load("A" if o else "S", "st_y", T.y[:, ALL * o + ALL - M:ALL * o + ALL], T.yt[:, ALL * o + ALL - M:ALL * o + ALL], r=["yt%d%d" % (R - 1, o)], w=["out.y%d" % o])
-    load("S", "st_mk", T.mk[0:1, :], T["mt%d" % (R % 2)][0:128:32, :], r=["mt%d" % (R % 2)], w=["out.mk"])
+    load("S", "st_mk", T.mk[0:1, :], T["mk%d" % (R % 2)][:, 30:32], r=["mk%d.0" % (R % 2), "mk%d.1" % (R % 2)], w=["out.mk"])
     op("S", "end", None, r=["out.sel%d" % t for t in range(R)] + ["out.oca", "out.oc", "out.ya0", "out.ya1", "out.y0", "out.y1", "out.mk"]
        + ["out.osc%d" % k for k in range(4)])
     _emit(P, g, T)

from concourse.bass import DstId, RemoteDMATransfer
from concourse.mybir import dt, AluOpType as ALU, ActivationFunctionType as AF

M, R, O = 16, 3, 2
HELPERS = 2
FUSE = False
TOK, CAND = 24, 96
RELAY = {"ca": (2,)}
BFT, F32, I32, U16, COD, PLN = "bfloat16", "float32", "int32", "uint16", "float8_e4m3fn_x4", "uint8"
SCRATCH = {}


def _sb(name, n, d):
    SCRATCH[name] = ("sbuf", [128, n], d)


def _codes(name, n):
    _sb(name + "q", n, COD)
    _sb(name + "s", n, PLN)


for _n, _w in (("ctile", 512), ("zt", 516), ("xt", 1024), ("wt", 1024), ("h", 512), ("ind", 512),
               ("ones", 128), ("ident", 128), ("sg", 128), ("csum", 256), ("over", 512), ("junk0", 256), ("junk1", 256), ("junk2", 512), ("junk3", 128)):
    _sb(_n, _w, BFT)
for _n, _w in (("mrow", 256), ("d0", 256), ("d1", 256), ("run0", 256), ("run1", 256), ("fac", 80), ("low", 16), ("sq", 128),
               ("bc", 64), ("mtb", 64), ("v16", 16), ("vrow", 80), ("vblk", 160), ("vtr", 160), ("yt", 96), ("name", 2),
               ("ks", 80), ("krow", 256), ("kinit", 2), ("num", 2), ("rk", 4), ("won", 2), ("selc", R),
               ("place", 64), ("rest", 128), ("hit", 128), ("hitt", 128), ("pair", 128), ("part", 2)):
    _sb(_n, _w, F32)
for _t in range(2):
    _sb("mk%d" % _t, 32, F32)
for _n, _w in (("pn", 2), ("pl", 2), ("vi", 80), ("vi2", 80), ("xi", 16)):
    _sb(_n, _w, I32)
_sb("pl2", 1, F32)
_sb("offx", 16, U16)
_sb("offu", 8, U16)
_sb("offv", 6, U16)
_sb("offo", 2, U16)
_sb("offi", 2, U16)
for _t in range(R):
    _sb("off%d" % _t, 4, U16)
    _sb("land%d" % _t, 80, BFT)
    _codes("win%d" % _t, 128)
    _codes("v%d" % _t, 128)
for _n, _w in (("c", 128), ("call", 256), ("x", 256), ("xu", 256), ("w", 256), ("vu", 128), ("ub", 128), ("vo", 48), ("ind", 128), ("eb", 512)):
    _codes(_n, _w)
for _b in range(8):
    SCRATCH["ps%d" % _b] = ("psum", [128, 512], F32)
SEMAPHORES = ["rc", "ra", "rb"] + ["r%s%d" % (k, t) for k in "nqs" for t in range(R)] + ["ls"] + ["e%d" % i for i in range(130)]


TOGETHER = {"above": "ind", "neg": "ind", "key": "key", "row": "row", "half1": "row", "next": "next", "hit0": "hit0", "hit1": "hit1",
            "part0": "sum0", "pair0": "sum0", "part1": "sum1", "pair1": "sum1", "offt": "offt", "offc": "offc", "vinq": "vinq", "vins": "vins",
            "rec": "rec", "spa0": "spa0", "spa1": "spa1", "spa2": "spa2", "spa3": "spa3", "bc": "bc", "ub": "ub", "sum": "sum", "xu0": "xu0", "xu1": "xu1", "turnw": "turnw", "vblk": "vblk", "qeb": "qeb"}


def _add(P, q, name, fn, r=(), w=(), inc=1, ext=None):
    ops, tags = P["ops"], P["tags"]
    i = len(ops)
    deps = set()
    if q == "G" and name[:3] != "snd":
        w = list(w) + ["pool"]
    for t in r:
        s = tags.setdefault(t, {"w": None, "r": []})
        if s["w"] is not None:
            deps.add(s["w"])
        if t[0] == "B":
            deps.update(j for j in s["r"] if ops[j]["q"] != q)
    for t in w:
        s = tags.setdefault(t, {"w": None, "r": []})
        if s["w"] is not None:
            deps.add(s["w"])
        deps.update(s["r"])
    for t in r:
        tags[t]["r"].append(i)
    for t in w:
        tags[t]["w"] = i
        tags[t]["r"] = []
    deps.discard(i)
    ops.append({"q": q, "name": name, "fn": fn, "deps": deps, "inc": inc, "ext": ext, "set": P["set"] if ext is None and inc == 1 else None})


def _emit(P, g, T):
    queues = {"G": g, "V": g.vector, "A": g.scalar, "P": g.tensor, "S": g.sync}
    ops = P["ops"]
    known = {q: 0 for q in queues}
    sets = {}
    for i, o in enumerate(ops):
        if o["set"] is not None:
            sets.setdefault(o["set"], []).append(i)
    done, whole, waits, used = [], [], [], set()
    for i, o in enumerate(ops):
        if o["ext"] is not None:
            done.append(1 << i)
            whole.append(1 << i)
            waits.append([])
            continue
        need = []
        open_ = [j for j in o["deps"] if not known[o["q"]] >> j & 1]
        for j in sorted({sets[ops[j]["set"]][-1] if ops[j]["set"] is not None else j for j in open_}, reverse=True):
            assert j < i, (o["name"], ops[j]["name"])
            if whole[j] & ~known[o["q"]]:
                need.append(j)
                known[o["q"]] |= whole[j]
        keep = [j for j in need if any(whole[j] >> d & 1 and not any(whole[m] >> d & 1 for m in need if m != j) for d in open_)]
        left = [d for d in open_ if not any(whole[m] >> d & 1 for m in keep)]
        keep += [j for j in need if j not in keep and any(whole[j] >> d & 1 for d in left)]
        waits.append(sorted(keep, key=lambda j: (ops[j]["ext"] is not None, j)))
        used.update(keep)
        done.append(known[o["q"]] | 1 << i)
        w = 0
        for j in (sets[o["set"]] if o["set"] is not None else [i]):
            w |= done[j] if j <= i else 0
        whole.append(w)
    pool, val, taken = [], {}, {}
    for i, o in enumerate(ops):
        if o["ext"] is not None:
            val[i] = o["ext"]
            continue
        q = queues[o["q"]]
        for j in waits[i]:
            q.wait_ge(*val[j])
        if o["fn"] is None:
            continue
        ins = o["fn"](q)
        mates = sets[o["set"]] if o["set"] is not None else [i]
        if mates[-1] in used:
            dma = o["inc"] > 1
            if i == mates[0]:
                free = [s for s in pool if not dma and not s["dma"] and all(done[j] & s["last"] == s["last"] for j in mates)]
                free.sort(key=lambda s: -s["last"])
                if free:
                    s = free[0]
                else:
                    s = {"sem": T.sem["e%d" % len(pool)], "n": 0, "dma": dma}
                    pool.append(s)
                s["last"] = sum(1 << j for j in mates)
                taken[mates[0]] = s
            s = taken[mates[0]]
            s["n"] += o["inc"]
            ins.then_inc(s["sem"], o["inc"])
            val[i] = (s["sem"], s["n"])


def _count(mask):
    return bin(mask).count("1")


def _ways(cores, r, topo):
    chip = [topo.chip(q) for q in cores]
    ways = {"far": [], "plane": [], "mate": []}
    for d in range(1, len(cores)):
        q = r ^ d
        way = "mate" if topo.mates(chip[r], chip[q]) else "plane" if topo.same_plane(chip[r], chip[q]) else "far"
        ways[way].append(q)
    plane = list(ways["plane"])
    others = []
    while ways["far"] or ways["plane"]:
        for way in ("far", "plane"):
            others += ways[way][:1]
            del ways[way][:1]
    others += ways["mate"]
    me = cores[r]
    helpers = [c for c in topo.cores_of(me) if c not in cores and topo.die(c) == topo.die(me)]
    reach = {c: [q for q in others if topo.may_write(c, cores[q])] for c in helpers}
    helpers = sorted(helpers, key=lambda c: len(reach[c]))
    helpers = [helpers[0], helpers[-1]][:HELPERS]
    far = near = -1
    for q in others:
        far &= topo.mask(me, cores[q])
    for c in helpers:
        near &= topo.mask(me, c)
    return others, [reach[c] for c in helpers], helpers, far, near & ~far


def _dst(topo, c):
    rid, pid, _ = topo.addr(c)
    return DstId(rid=rid, pnc=pid)


def _u8(ap):
    return ap.bitcast(dt.uint8)


def _slot(src, dst, n):
    return (src - dst) % n


def _pieces(T, r, others, plane):
    n = len(others) + 1
    half = [q for q in others if 2 * q // n == 2 * r // n]
    raw = [("cq", _u8(T.cq[:, 0:32]), lambda q: _u8(T.callq[:, 32 * r:32 * r + 32]), "rc", others),
           ("ca", T.cs[:, 0:32], lambda q: T.calls[:, 32 * r:32 * r + 32], "ra", [q for q in others if q not in half]),
           ("cb", T.cs[:, 0:32], lambda q: T.calls[:, 32 * r:32 * r + 32], "rb", half)]
    for t in range(R):
        wq, ws = T["win%dq" % t], T["win%ds" % t]
        raw.append(("tq%d" % t, _u8(wq[:, TOK:TOK + 8]), lambda q, w=wq: _u8(w[:, TOK + 8 * _slot(r, q, n):TOK + 8 * _slot(r, q, n) + 8]), "rq%d" % t, others))
        raw.append(("ts%d" % t, ws[:, TOK:TOK + 8], lambda q, w=ws: w[:, TOK + 8 * _slot(r, q, n):TOK + 8 * _slot(r, q, n) + 8], "rs%d" % t, others))
    out = {}
    for kind, src, dst, sem, to in raw:
        shares = []
        for k, reach in zip(RELAY.get(kind, ()), plane):
            shares.append([q for q in reach if q in to and not any(q in s for s in shares)][:k])
        out[kind] = (src, dst, sem, [q for q in to if not any(q in s for s in shares)], shares)
    return out


def _helper(g, core, T, topo, cores, r):
    others, plane, helpers, far, near = _ways(cores, r, topo)
    j = helpers.index(core)
    sent = 0
    for src, dst, sem, direct, shares in _pieces(T, r, others, plane).values():
        share = shares[j] if j < len(shares) else []
        if not share:
            continue
        mask = far
        for q in share:
            mask &= topo.mask(core, cores[q])
        g.wait_ge(T.sem[sem], _count(near))
        g.remote_dma_fused([RemoteDMATransfer(dst_ids=[_dst(topo, cores[q]) for q in share], dma_engine_mask=mask, remote_sem=T.sem[sem],
                                              srcs=[src], dsts=[dst(q) for q in share])], local_sem=T.sem.ls)
        sent += _count(mask)
    if sent:
        g.wait_ge(T.sem.ls, sent)


def rank_program(g, core, T, topo):
    cores = list(T.cores)
    N = len(cores)
    r = T.rank_of(core)
    if r is None:
        for q in range(N):
            if core in _ways(cores, q, topo)[2]:
                _helper(g, core, T, topo, cores, q)
        return
    P = {"ops": [], "tags": {}, "set": None, "turn": -1}
    others, plane, helpers, mask, near = _ways(cores, r, topo)
    lanes = _count(mask)
    sent = [0]
    piece = _pieces(T, r, others, plane)

    def op(q, name, *a, **k):
        P["set"] = (TOGETHER[name], P["turn"]) if name in TOGETHER else None
        _add(P, q, name, *a, **k)

    u8 = _u8

    def w32(ap):
        return ap.bitcast(dt.uint32)

    def slot(src, dst):
        return _slot(src, dst, N)

    def send(name, reads, src, dst, sem, direct, shares=(), beside=None):
        tr = []
        if direct:
            tr.append(RemoteDMATransfer(dst_ids=[_dst(topo, cores[q]) for q in direct], dma_engine_mask=mask, remote_sem=T.sem[sem],
                                        srcs=[src], dsts=[dst(q) for q in direct]))
            sent[0] += lanes
        via = [c for c, s in zip(helpers, beside[1][4]) if s] if beside else []
        if via:
            tr.append(RemoteDMATransfer(dst_ids=[_dst(topo, c) for c in via], dma_engine_mask=near, remote_sem=T.sem[beside[1][2]],
                                        srcs=[beside[0]], dsts=[beside[0] for c in via]))
            sent[0] += _count(near)
        if tr:
            op("G", name, lambda e: e.remote_dma_fused(tr, local_sem=T.sem.ls), r=reads)

    def arrive(tag, sem, senders):
        op("X", "arr", None, w=[tag], ext=(T.sem[sem], lanes * senders))

    def memset(name, ap, v, w):
        op("V", name, lambda e: e.memset(ap, v), w=w)

    def quant(name, out, c0, tile, a, n, r, w):
        op("V", name, lambda e: e.quantize_mx(T[out + "q"][:, c0:c0 + n], T[out + "s"][:, c0:c0 + n], T[tile][:, a:a + 4 * n]), r=r, w=w)

    def mm(name, bank, st, a, mv, b, n, r, start=True, stop=True):
        op("P", name, lambda e: e.matmul_mx(T["ps%d" % bank][:, 0:n], T[st + "q"][:, a:a + 128], T[st + "s"][:, a:a + 128],
                                            T[mv + "q"][:, b:b + n], T[mv + "s"][:, b:b + n], start, stop), r=r, w=["B%d" % bank])

    def ps(bank, a, b):
        return T["ps%d" % bank][:, a:b]

    def ts(name, out, in0, s1, s2, o0, o1, r, w):
        if o1 is None:
            op("V", name, lambda e: e.tensor_scalar(out, in0, s1, None, o0), r=r, w=w)
        else:
            op("V", name, lambda e: e.tensor_scalar(out, in0, s1, s2, o0, o1), r=r, w=w)

    def tt(name, out, in0, in1, o, r, w):
        op("V", name, lambda e: e.tensor_tensor(out, in0, in1, o), r=r, w=w)

    def scan(name, out, d0, d1, first, o0, o1, r, w):
        op("V", name, lambda e: e.tensor_tensor_scan(out, d0, d1, first, o0, o1), r=r, w=w)

    def flip(name, out, in_, r, w):
        op("V", name, lambda e: e.transpose(out, in_), r=r, w=w)

    def vcopy(name, out, in_, r, w):
        op("V", name, lambda e: e.tensor_copy(out, in_), r=r, w=w)

    def acopy(name, out, in_, r, w, **k):
        op("A", name, lambda e: e.activation(out, in_, AF.Copy, **k), r=r, w=w)

    def ramp(name, out, n, first, step, r, w):
        op("A", name, lambda e: e.activation(out, T.v16[:, 0:n], AF.Identity, bias=float(first), scale=float(step)), r=["v16"] + r, w=w)

    def fill(name, out, n, v, w):
        op("A", name, lambda e: e.activation(out, T.ones[:, 0:n], AF.Identity, bias=float(v), scale=0.0), r=["ones"], w=w)

    def load(q, name, out, in_, r=(), w=()):
        op(q, name, lambda e: e.dma_start(out, in_), r=r, w=w, inc=16)

    def runs(v):
        cuts = [0] + [k for k in range(1, len(v)) if v[k] != v[k - 1] - 1] + [len(v)]
        return list(zip(cuts, cuts[1:]))

    order = [None] * M
    for k in range(M):
        i, h = (r - k) % N, k // N
        order[(i % 4) + 4 * h + 8 * (1 - i // 4)] = k
    HT = ["h0", "h1", "h2", "h3"]
    EB = ["eb0", "eb1", "eb2", "eb3"]
    VIN = ["vin.q0", "vin.q2", "vin.s0", "vin.s2"]
    CV = 96
    NV = 5 * M
    OWN = 2 * N
    HB = 2 * r // N
    ALL = R * M
    NAMING = ((0, 0, 0), (0, 1, 0), (1, 0, 0), (0, 0, 128), (1, 1, 0), (0, 1, 128), (1, 0, 128), (1, 1, 128))

    load("S", "ldc", T.ctile[:, 0:128], T.c[:, :], w=["ctile"])
    load("S", "ldu", T.h[:, 4 * NV:4 * NV + 16], T.u[:, :], w=["hu"])
    for j in range(2):
        load("S", "ldx", T.xt[:, 512 * j:512 * j + 512], T.x[:, 512 * j:512 * j + 512], w=["xt%d" % j])
    memset("ms_ones", T.ones[:], 1.0, ["ones"])
    memset("ms_c", T.ctile[:, 128:512], 0.0, ["ctile0"])
    op("G", "pn", lambda e: e.iota(T.pn[:], [[128, 2]], 0, 1), w=["pn"])
    op("G", "xi", lambda e: e.iota(T.xi[:], [[1, 2], [32, 8]], 0, 0), w=["xi"])
    op("G", "v16", lambda e: e.iota(T.v16[:], [[1, 16]], 0, 0, allow_small_or_imprecise_dtypes=True), w=["v16"])
    memset("ms_h", T.h[:, 4 * NV + 16:512], 0.0, ["hc0", "hc1"])
    ts("pl", T.pl[:], T.pn[:], 15, None, ALU.bitwise_and, None, ["pn"], ["pl"])
    memset("ms_h", T.h[:, 0:4 * NV], 0.0, HT)
    for j in range(2):
        ts("offi", T.offi[:, j:j + 1], T.pl[:, 0:1], 16.0 * j, None, ALU.add, None, ["pl"], ["offi%d" % j])
    memset("ms_h1", T.h[:, 4 * CV:4 * CV + 2], 1.0, ["hc0"])
    memset("ms_h2", T.h[:, 4 * CV + 6:4 * CV + 8], 1.0, ["hc1"])
    memset("offu", T.offu[:], NV, ["offu"])
    ts("pl2", T.pl2[:], T.pl[:, 0:1], 2.0, None, ALU.mult, None, ["pl"], ["pl2"])

    quant("qc", "c", 0, "ctile", 0, 128, ["ctile", "ctile0"], ["c"])
    send("snd_c", ["c"], *piece["cq"])
    LATE = bool(RELAY.get("ca"))
    early, late = ("cb", "ca") if LATE else ("ca", "cb")
    send("snd_c", ["c"], *piece[early], beside=(piece[late][0], piece[late]))
    send("snd_c", ["c"], *piece[late])
    arrive("call.q", "rc", N - 1)
    arrive("call.a", "ra", N // 2)
    arrive("call.b", "rb", N // 2 - 1)
    CALL = ["call.q", "call.a", "call.b", "own.q", "own.s"]

    op("G", "vi", lambda e: e.iota(T.vi[:], [[4, 2], [8, 8], [9, 5]], 128 - 9 - 8 * r, 0), w=["vi"])
    op("G", "ident", lambda e: e.affine_select(T.ident[:], T.ones[:], [[-1, 128]], ALU.is_equal, 0.0, 0, 1), r=["ones"], w=["ident"])
    fill("fac", T.fac[:], NV, 0.5, ["fac0", "fac1"])
    fill("low", T.low[:], M, -1e29, ["low"])
    for j in range(2):
        fill("fac", T.fac[:, j:NV:5], M, float(j), ["fac%d" % j])
    fill("land", T.land0[:, OWN:], 64, 0.0, ["cnt0"])
    quant("qv", "vu", 0, "h", 0, 128, HT + ["hu", "hc0", "hc1"], VIN)
    op("V", "ownq", lambda e: e.tensor_copy(w32(T.callq[:, 32 * r:32 * r + 32]), w32(T.cq[:, 0:32]).indirect(T.offi[:, 0:2])), r=["c", "offi0", "offi1"], w=["own.q"])
    op("A", "owns", lambda e: e.activation(T.calls[:, 32 * r:32 * r + 32], T.cs[:, 0:32].indirect(T.offi[:, 0:2]), AF.Copy), r=["c", "offi0", "offi1"], w=["own.s"])
    op("V", "ub", lambda e: e.tensor_copy(w32(T.ubq[:, 0:128]), w32(T.vuq[:, 0:128]).indirect(T.offu[:, 0:8])), r=VIN + ["offu"], w=["ub.q"])
    op("A", "ub", lambda e: e.activation(T.ubs[:, 0:128], T.vus[:, 0:128].indirect(T.offu[:, 0:8]), AF.Copy), r=VIN + ["offu"], w=["ub.s"])
    for j in range(2):
        quant("qx", "x", 128 * j, "xt", 512 * j, 128, ["xt%d" % j], ["x%d" % j])
    X = ["x0", "x1"]
    mm("m0", 6, "ub", 0, "x", 0, 256, X + ["ub.q", "ub.s"])
    ts("offx", T.offx[:], T.xi[:], T.pl2[:], None, ALU.add, None, ["xi", "pl2"], ["offx"])
    acopy("m0", T.mrow[:], ps(6, 0, 256), ["B6"], ["mrow%d.%d" % (a, q) for a in range(4) for q in range(4)])
    for b in range(2):
        op("V", "xu%d" % b, lambda e, b=b: e.tensor_copy(w32(T.xuq[:, 128 * b:128 * b + 128]), w32(T.xq[:, 0:256]).indirect(T.offx[:, 8 * b:8 * b + 8])),
           r=X + ["offx"], w=["xu.q%d" % b])
        op("A", "xu%d" % b, lambda e, b=b: e.activation(T.xus[:, 128 * b:128 * b + 128], T.xs[:, 0:256].indirect(T.offx[:, 8 * b:8 * b + 8]), AF.Copy),
           r=X + ["offx"], w=["xu.s%d" % b])
    vcopy("num", T.num[:], T.pn[:], ["pn"], ["num"])
    ts("kinit", T.kinit[:], T.pn[:], -1.0 / 256, 255.0 / 256, ALU.mult, ALU.add, ["pn"], ["kinit"])
    PT, PC = [], ["placec0", "placec1"]

    def places():
        for a, b in runs(order):
            PT.append("placet%d" % a)
            ramp("place", T.place[:, a:b], b - a, 255 - 2 * order[a], 2, [], PT[-1:])
        for j in range(2):
            ramp("place", T.place[:, M * j + 32:M * j + 32 + M], M, 255, -2, [], [PC[j]])
        acopy("place", T.place[:, M:2 * M], T.place[:, 0:M], list(PT), ["placet."])
        PT.append("placet.")

    def remaking_list():
        ramp("vrowk", T.vrow[:, 0:NV:5], M, CAND, 1, ["vrow"], ["vrow"])
        for c in range(5):
            for b in range(2):
                acopy("vblk", T.vblk[:, 32 * c + 16 * b:32 * c + 16 * b + 16], T.vrow[:, 16 * c:16 * c + 16], ["vrow"], ["vblk%d%d" % (c, b)])

    def remaking_offsets():
        flip("vtr", T.vtr[:], T.vblk[:], ["vblk%d%d" % (c, b) for c in range(5) for b in range(2)], ["vtr"])
        ts("offo", T.offo[:], T.pl[:], 5.0, 4.0, ALU.mult, ALU.add, ["pl"], ["offo"])
        vcopy("offv", T.offv[:, 0:5], T.vtr[:, 0:160:32], ["vtr"], ["offv"])

    def one_hot(bb):
        for b in bb:
            quant("qeb", "eb", 128 * b, "zt", 3 - b, 128, ["zt"], [EB[b]])

    def zmul(v):
        for b in range(2):
            mm("z%d" % b, 4 + b, "xu", 128 * b, v, 0, 128, ["xu.q%d" % b, "xu.s%d" % b] + (VIN if v == "vu" else [v]))

    def mk(t, b):
        return T["mk%d" % (t % 2)][:, 30 + b:31 + b]

    def marks(t, b):
        q = "mk%d.%d" % (t % 2, b)
        if t == 0:
            vcopy("mark%d" % b, mk(0, b), ps(4 + b, NV, NV + 1), ["B%d" % (4 + b)], [q])
        else:
            scan("mark%d" % b, T["mk%d" % (t % 2)][:, b:2 * M:2], T["ps%d" % (4 + b)][:, 4:NV:5], T.low[:], mk(t - 1, b),
                 ALU.max, ALU.max, ["B%d" % (4 + b), "low", "mk%d.%d" % ((t - 1) % 2, b)], [q])

    def turn(t):
        for b in range(2):
            flip("turnw", T.mtb[:, b:64:2], T.bc[:, 32 * b:32 * b + 32], ["bc%d" % b], ["mtb%d" % b])

    def spread(t, aa):
        for a in aa:
            op("G", "spread%d" % a, lambda e, a=a: e.partition_broadcast(T.mrow[:, 64 * a:64 * a + 64], T.mtb[32 * a:32 * a + 1, :], 128),
               r=["mtb0", "mtb1"], w=["mrow%d.%d" % (a, q) for q in range(4)])

    def widen(t):
        for b in range(2):
            acopy("bc", T.bc[:, 32 * b:32 * b + 32], T.ones[:, 0:32], ["ones", "mk%d.%d" % (t % 2, b)], ["bc%d" % b], scale=mk(t, b))

    def spread_a(aa):
        for a in aa:
            for q in range(4):
                acopy("spa%d" % a, T.mrow[32 * q:32 * q + 32, 64 * a:64 * a + 64], T.mtb[32 * a:32 * a + 32, :], ["mtb0", "mtb1"], ["mrow%d.%d" % (a, q)])

    zmul("vu")
    ts("vi2", T.vi2[:], T.vi[:], 63, None, ALU.bitwise_and, None, ["vi"], ["vi2"])
    memset("ms_zt", T.zt[:], 0.0, ["zt"])
    ts("vrow", T.vrow[:], T.vi2[:], float(TOK), None, ALU.add, None, ["vi2"], ["vrow"])
    marks(0, 0)
    marks(0, 1)
    places()
    acopy("eb", T.zt[:, 3:515:4], T.ident[:], ["ident"], ["zt"], scale=0.5)
    remaking_list()
    for t in range(R if FUSE else 0):
        op("V", "padq", lambda e, t=t: e.tensor_copy(w32(T["win%dq" % t][:, 0:16]), w32(T.xq[:, 0:256]).indirect(T.offi[:, 0:1])), r=X + ["offi0"], w=["win%d.pq" % t])
        op("A", "pads", lambda e, t=t: e.activation(T["win%ds" % t][:, 0:16], T.xs[:, 0:256].indirect(T.offi[:, 0:1]), AF.Copy), r=X + ["offi0"], w=["win%d.ps" % t])

    def above(t, b, k):
        ts("above", T.ind[:, 2 * k + b:512:4], ps(b, 128 * k, 128 * k + 128), mk(t, b), None, ALU.is_gt, None,
           ["B%d" % b, "mk%d.%d" % (t % 2, b)], ["ind%d%d" % (b, k)])

    def above_a(t):
        for a in (0, 64):
            op("A", "sgn", lambda e, a=a: e.activation(T.sg[:, a:a + 64], T.sq[:, a:a + 64], AF.Sign, bias=mk(t, 0), scale=-1.0),
               r=["sq0", "mk%d.0" % (t % 2)], w=["sg%d" % a])

    def above_b(t):
        for a in (0, 64):
            op("A", "neg", lambda e, a=a: e.activation(T.ind[:, 2 - 2 * HB + 4 * a:4 * a + 256:4], T.sg[:, a:a + 64], AF.Relu, scale=-1.0),
               r=["sg%d" % a], w=["ind0%d%s" % (1 - HB, "." if a else "")])

    def pieces(what, b, lo, hi):
        return ["%s%d.%d" % (what, b, h) for h in range(lo // 64, hi // 64)]

    def name_diff(b, lo, hi):
        tt("diff%d" % b, T["d%d" % b][:, lo:hi], ps(2 + b, lo, hi), T.mrow[:, lo:hi], ALU.subtract,
           ["B%d" % (2 + b)] + ["mrow%d.%d" % (a, q) for a in range(lo // 64, hi // 64) for q in range(4)], pieces("d", b, lo, hi))

    def name_run(b, lo, hi):
        scan("run%d" % b, T["run%d" % b][:, lo:hi], T["d%d" % b][:, lo:hi], T["d%d" % b][:, lo:hi], T["run%d" % b][:, lo - 1:lo] if lo else -1e29,
             ALU.max, ALU.max, pieces("d", b, lo, hi) + (pieces("run", b, 0, lo) if lo else []), pieces("run", b, lo, hi))

    def name_at(b):
        op("A", "name%d" % b, lambda e: e.activation(T["junk%d" % b][:], T["run%d" % b][:], AF.Sign, bias=T["run%d" % b][:, 255:256], scale=-1.0,
                                                     accum_out=T.name[:, b:b + 1]), r=pieces("run", b, 0, 256), w=["junk%d" % b, "name%d" % b])

    def count_sums(b1, b2):
        for b, a, tags in ((b1, 0, ["over0"]), (b2, 256, ["over10", "over11"])):
            scan("sum", T.csum[:, b:256:2], T.over[:, a:a + 128], T.over[:, a + 128:a + 256], 0.0, ALU.add, ALU.add, tags, ["csum%d" % b])

    def pick_out(t):
        v = "v%d" % t
        op("V", "outq", lambda e: e.tensor_copy(w32(T.voq[:, M * t:M * t + M]), w32(T[v + "q"][:, 0:128]).indirect(T.offo[:, 0:1])), r=[v, "offo"], w=["vo.q%d" % t])
        op("A", "outs", lambda e: e.activation(T.vos[:, M * t:M * t + M], T[v + "s"][:, 0:128].indirect(T.offo[:, 0:1]), AF.Copy), r=[v, "offo"], w=["vo.s%d" % t])

    def products(t):
        v = "v%d" % t
        for o in range(O):
            mm("y%d" % o, 6 + o, "w", 128 * o, v, 0, 128, ["w", v])

    def product_copies(t):
        for o in range(O):
            acopy("yc%d" % o, T.yt[:, ALL * o + M * t:ALL * o + M * t + M], T["ps%d" % (6 + o)][:, 4:NV:5], ["B%d" % (6 + o)], ["yt%d%d" % (t, o)])

    def rank(b, h):
        j = 2 * h + b
        op("A", "rank", lambda e: e.activation(T.junk2[:, 128 * j:128 * j + 128], T.krow[:, 128 * h:128 * h + 128], AF.Sign, bias=T.ks[:, 40 - b:41 - b],
                                               scale=-1.0, accum_out=T.rk[:, j:j + 1]),
           r=["ks%d" % b] + (["next%d.%d" % (q, d) for q in range(4) for d in (1, 3)] if h else ["row", "half0", "half1"]), w=["junk2.%d" % j, "rk%d" % j])

    def rest(b, tags):
        ts("rest", T.rest[:, 64 * b:64 * b + 64], T.place[:], T.rk[:, b:b + 1], None, ALU.subtract, None, tags + ["rk%d" % b], ["rest%d" % b])

    def hit(j, b):
        a = 64 * j + 32 * b
        ts("hit%d" % j, T.hit[:, a:a + 32], T.rest[:, 64 * b + 32 * j:64 * b + 32 * j + 32], T.rk[:, 2 + b:3 + b], (T.num if j else T.name)[:, b:b + 1],
           ALU.is_equal, ALU.mult, ["rest%d" % b, "rk%d" % (2 + b), "num" if j else "name%d" % b], ["hit%d%d" % (j, b)])

    def hit_turn(j):
        flip("hitt", T.hitt[:, 64 * j:64 * j + 64], T.hit[:, 64 * j:64 * j + 64], ["hit%d0" % j, "hit%d1" % j], ["hitt%d" % j])

    def sums(j):
        c = slice(64 * j, 64 * j + 64)
        op("A", "part%d" % j, lambda e: e.activation(T.junk3[:, c], T.hitt[:, c], AF.Copy, accum_out=T.part[:, j:j + 1]), r=["hitt%d" % j], w=["junk3%d" % j, "part%d" % j])
        for q in range(2):
            a = 32 * (1 - q)
            scan("pair%d" % j, T.pair[32 * q:32 * q + 32, c], T.hitt[a:a + 32, c], T.hitt[a + 64:a + 96, c], 0.0, ALU.add, ALU.add, ["hitt%d" % j], ["pair%d%d" % (j, q)])

    def total(j, name, out, w):
        ts(name, out, T.part[0:64, j:j + 1], T.part[64:128, j:j + 1], T.pair[0:64, 64 * j + 63:64 * j + 64], ALU.add, ALU.add,
           ["part%d" % j, "pair%d0" % j, "pair%d1" % j], w)

    def one_round(t):
        win, off, cnt, land = "win%d" % t, "off%d" % t, "cnt%d" % t, "land%d" % t
        P["turn"] = t
        if t == 0:
            b1, b2 = (HB, 1 - HB) if LATE else (1 - HB, HB)
            need = {HB: ["call.q", "call.b", "own.q", "own.s"], 1 - HB: ["call.q", "call.a"]}
            MR = ["mrow%d.%d" % (a, q) for a in range(4) for q in range(4)]
            mm("sa", 2 + b1, "call", 128 * b1, "x", 0, 256, X + need[b1])
            tt("over", T.over[:, 0:256], ps(2 + b1, 0, 256), T.mrow[:], ALU.is_gt, ["B%d" % (2 + b1)] + MR, ["over0"])
            for j in range(2):
                mm("sa", 4 + j, "call", 128 * b2, "x", 128 * j, 128, X + need[b2])
            mm("sa", 2 + b2, "call", 128 * b2, "x", 0, 256, X + need[b2])
            for j in range(2):
                tt("over", T.over[:, 256 + 128 * j:384 + 128 * j], ps(4 + j, 0, 128), T.mrow[:, 128 * j:128 * j + 128], ALU.is_gt, ["B%d" % (4 + j)] + MR, ["over1%d" % j])
            count_sums(b1, b2)
            own, tags = T.csum[:, 254:256], ["csum0", "csum1"]
            acopy("cnt", T[land][:, OWN:OWN + 2], own, tags, [cnt])
        else:
            marks(t, 0)
            above_a(t)
            marks(t, 1)
            above(t, 0, HB)
            above(t, 1, HB)
            above(t, 1, 1 - HB)
            widen(t)
            above_b(t)
            turn(t)
            quant("qind", "ind", 0, "ind", 0, 128, ["ind00", "ind01", "ind10", "ind11", "ind0%d." % (1 - HB)], ["indq"])
            spread(t, (0,))
            spread_a((1, 2, 3))
            mm("cnt", 6, "ind", 0, "vu", 0, 128, ["indq"] + VIN)
            vcopy("cnt", T[land][:, OWN:OWN + 2], ps(6, CV, CV + 2), ["B6"], [cnt])
            own, tags = T[land][:, OWN:OWN + 2], [cnt]
        send("snd_n", tags, own, lambda q: T[land][:, 2 * slot(r, q):2 * slot(r, q) + 2], "rn%d" % t, others)
        arrive(land, "rn%d" % t, N - 1)
        if t == 0:
            for b in range(2):
                mm("sb", b, "xu", 128 * b, "call", 0, 256, ["xu.q%d" % b, "xu.s%d" % b] + CALL)
            acopy("sq", T.sq[:], ps(0, 128 - 128 * HB, 256 - 128 * HB), ["B0"], ["sq0"])
            for b in (b1, b2):
                name_diff(b, 0, 256)
            for b in (b1, b2):
                name_run(b, 0, 256)
        else:
            for f, b, lo in NAMING:
                (name_run if f else name_diff)(b, lo, lo + 128)
        for b in ((0, 1) if t else (b1, b2)):
            name_at(b)
        if t == 1:
            load("S", "ldw", T.wt[:, 512:1024], T.w[:, 512:1024], r=[land], w=["wt1"])
        for b in range(2):
            scan("key", T.ks[:, 1:40] if b else T.ks[:, 78:39:-1], T.ones[:, 0:N + 31], T[land][:, 2 + b:80:2], T.kinit[:, b:b + 1], ALU.mult, ALU.add,
                 [land, cnt, "ones", "kinit"], ["ks%d" % b])
        KS = ["ks0", "ks1"]
        flip("row", T.krow[:, 0:64], T.ks[:, 8:72], KS, ["row"])
        for h in (1, 0):
            flip("half%d" % h, T.krow[64 * h:64 * h + 64, 64:128], T.ks[64 - 64 * h:128 - 64 * h, 8:72], KS, ["half%d" % h])
        acopy("next", T.krow[96:128, 128:256], T.krow[64:96, 0:128], ["row", "half1"], ["next3.1", "next3.3"])
        for q in range(3):
            for d in (1, 3):
                flip("next", T.krow[32 * q:32 * q + 32, 96 + 32 * d:160 + 32 * d], T.ks[32 * (q ^ d):32 * (q ^ d) + 32, 8:72], KS, ["next%d.%d" % (q, d)])
        for h in range(2):
            for b in range(2):
                rank(b, h)
        for b in range(2):
            rest(b, PT + PC)
        for j, b in ((0, 0), (1, 0), (0, 1), (1, 1)):
            hit(j, b)
        for j in range(2):
            hit_turn(j)
        for j in range(2):
            sums(j)
        for h in range(2):
            total(0, "offt", T[off][64 * h:64 * h + 64, 0:1], [off + "t%d" % h])
        for h in range(2):
            total(1, "offc", T[off][64 * h:64 * h + 64, 2:3], [off + "c%d" % h])
        OT = [off + "t0", off + "t1"]
        op("V", "tokq", lambda e: e.tensor_copy(w32(T[win + "q"][:, 16:32]), w32(T.xq[:, 0:256]).indirect(T[off][:, 0:1])), r=X + OT, w=[win + ".tq"])
        op("A", "toks", lambda e: e.activation(T[win + "s"][:, 16:32], T.xs[:, 0:256].indirect(T[off][:, 0:1]), AF.Copy), r=X + OT, w=[win + ".ts"])
        if FUSE:
            send("snd_tq", [win + ".tq", win + ".ts", win + ".ps"], *piece["tq%d" % t], beside=(T[win + "s"][:, 0:32], piece["ts%d" % t]))
            send("snd_ts", [win + ".ts"], *piece["ts%d" % t])
        else:
            send("snd_tq", [win + ".tq"], *piece["tq%d" % t])
            send("snd_ts", [win + ".ts"], *piece["ts%d" % t], beside=(piece["ts%d" % t][0], piece["ts%d" % t]))
        arrive("landq" + win, "rq%d" % t, N - 1)
        arrive("lands" + win, "rs%d" % t, N - 1)
        if t + 1 < R:
            tt("won", T.won[:], T.rk[:, 0:2], T.rk[:, 2:4], ALU.add, ["rk0", "rk1", "rk2", "rk3"], ["won"])
        OC = [off + "c0", off + "c1"]
        op("V", "candq", lambda e: e.tensor_copy(w32(T[win + "q"][:, CAND:CAND + M]), w32(T.callq[:, 0:256]).indirect(T[off][:, 2:3])), r=CALL + OC, w=[win + ".cq"])
        total(1, "selc", T.selc[0:64, t:t + 1], ["selc%d" % t])
        if t + 1 < R:
            ts("won", T.won[:], T.won[:], 255.0 - 2 * M + 1, -4096.0, ALU.is_gt, ALU.mult, ["won"], ["won"])
        op("A", "cands", lambda e: e.activation(T[win + "s"][:, CAND:CAND + M], T.calls[:, 0:256].indirect(T[off][:, 2:3]), AF.Copy), r=CALL + OC, w=[win + ".cs"])
        if t + 1 < R:
            tt("kinit", T.kinit[:], T.kinit[:], T.won[:], ALU.add, ["won", "kinit"], ["kinit"])
            fill("land", T["land%d" % (t + 1)][:, OWN:], 64, 0.0, ["cnt%d" % (t + 1)])
        if t == 0:
            remaking_offsets()
            one_hot((0, 1, 2, 3))
        if t == 1:
            quant("qw", "w", 0, "wt", 0, 256, ["wt0", "wt1"], ["w"])
        if t:
            pick_out(t - 1)
            products(t - 1)
            product_copies(t - 1)
        for a, b in ((0, 2), (2, 5)):
            op("V", "vinq", lambda e, a=a, b=b: e.tensor_copy(w32(T.vuq[:, 16 * a:16 * b]), w32(T[win + "q"][:, 0:128]).indirect(T.offv[:, a:b])),
               r=["landq" + win, win + ".tq", win + ".cq", win + ".pq", "offv"], w=["vin.q%d" % a])
        WS = ["lands" + win, win + ".ts", win + ".cs", win + ".ps", "offv"]
        op("A", "vins", lambda e: e.activation(T.vus[:, 0:32], T[win + "s"][:, 0:128].indirect(T.offv[:, 0:2]), AF.Copy), r=WS, w=["vin.s0"])
        op("V", "vins", lambda e: e.tensor_copy(T.vus[:, 32:80], T[win + "s"][:, 0:128].indirect(T.offv[:, 2:5])), r=WS, w=["vin.s2"])
        load("S", "st_sel", T.sel[0:1, M * t:M * t + M], T.selc[0:M, t:t + 1], r=["selc%d" % t, "lands" + win], w=["out.sel%d" % t])
        if t == 0:
            load("S", "ldw", T.wt[:, 0:512], T.w[:, 0:512], r=["lands" + win], w=["wt0"])
        if t == R - 1:
            for o in range(O):
                load("S", "st_y", T.y[:, ALL * o:ALL * o + M * t], T.yt[:, ALL * o:ALL * o + M * t], r=["yt%d%d" % (s, o) for s in range(t)], w=["out.ya%d" % o])
            load("S", "st_oc", T.oc[:, 0:4 * M * t], u8(T.voq[:, 0:M * t]), r=["vo.q%d" % s for s in range(t)], w=["out.oca"])
        for b in range(4):
            mm("dec%d" % b, 4 + b, "eb", 128 * b, "vu", 0, 128, [EB[b]] + VIN)
        for b in range(4):
            scan("rec", T.h[:, b:4 * NV:4], T.fac[:], ps(4 + b, 0, NV), 0.0, ALU.mult, ALU.add, ["B%d" % (4 + b), "fac0", "fac1"], ["h%d" % b])
        v = "v%d" % t
        quant("qv", v, 0, "h", 0, 128, HT + ["hu", "hc0", "hc1"], [v])
        if t == R - 1:
            products(t)
        zmul(v)

    for t in range(R):
        one_round(t)

    pick_out(R - 1)
    marks(R, 0)
    marks(R, 1)
    load("S", "st_oc", T.oc[:, 4 * (ALL - M):4 * ALL], u8(T.voq[:, ALL - M:ALL]), r=["vo.q%d" % (R - 1)], w=["out.oc"])
    for k in range(4):
        load("A" if k == 3 else "S", "st_osc%d" % k, T.osc[4 * k:4 * k + 4, :], T.vos[32 * k:32 * k + 4, 0:ALL], r=["vo.s%d" % t for t in range(R)], w=["out.osc%d" % k])
    product_copies(R - 1)
    for o in range(O):
        load("A" if o else "S", "st_y", T.y[:, ALL * o + ALL - M:ALL * o + ALL], T.yt[:, ALL * o + ALL - M:ALL * o + ALL], r=["yt%d%d" % (R - 1, o)], w=["out.y%d" % o])
    load("S", "st_mk", T.mk[0:1, :], T["mk%d" % (R % 2)][:, 30:32], r=["mk%d.0" % (R % 2), "mk%d.1" % (R % 2)], w=["out.mk"])
    op("S", "end", None, r=["out.sel%d" % t for t in range(R)] + ["out.oca", "out.oc", "out.ya0", "out.ya1", "out.y0", "out.y1", "out.mk"]
       + ["out.osc%d" % k for k in range(4)])
    _emit(P, g, T)
    g.wait_ge(T.sem.ls, sent[0])
